import numpy as np
import ml_dtypes


def mxq(x, axis, fmt="e4m3"):
    dtype, down = {"e4m3": (ml_dtypes.float8_e4m3fn, 7), "e5m2": (ml_dtypes.float8_e5m2, 14)}[fmt]
    v = np.moveaxis(np.asarray(x, np.float32).astype(ml_dtypes.bfloat16).astype(np.float64), axis, -1)
    blocks = v.reshape(v.shape[:-1] + (-1, 32))
    amax = np.abs(blocks).max(-1, keepdims=True)
    byte = np.maximum(np.where(amax > 0, np.frexp(amax)[1] - 1 + 127, 0) - down, 1)
    scale = np.exp2(byte - 127.0)
    codes = (blocks / scale).astype(np.float32).astype(dtype).astype(np.float64)
    return np.moveaxis((codes * scale).reshape(v.shape), -1, axis)


WIDE = False


def mx_kscale(k):
    if not WIDE:
        return np.ones(k)
    levels = np.array([10, -10, 5, -5, 0])
    if k % 512:
        return np.exp2(np.random.permutation(np.resize(levels, k // 32))).repeat(32)
    a = np.empty((k // 512, 16))
    for p in range(k // 512):
        a[p, :8] = np.random.permutation(np.resize(levels, 8))
        for g in range(8):
            far = levels[np.abs(levels - a[p, g]) >= 10]
            a[p, g + 8] = far[np.random.randint(len(far))]
    return np.exp2(a.ravel()).repeat(32)


def f64(x):
    return np.asarray(x).astype(np.float64)


def striped(idx):
    return np.tile(idx.reshape(-1, 16).T, (8, 1)).astype(np.uint16)


def unstriped(offs):
    return offs[:16].T.reshape(-1).astype(np.int64)


def pack_weight(w):
    k, n = w.shape
    w = f64(np.asarray(w, np.float32).astype(ml_dtypes.bfloat16)).reshape(k // 32, 32, n)
    amax = np.abs(w).max(1)
    byte = np.clip(np.where(amax > 0, np.frexp(amax)[1] - 1 + 127 - 7, 1), 1, 254)
    scaled = (w * np.exp2(127.0 - byte)[:, None, :]).reshape(k, n).astype(np.float32)
    words = np.ascontiguousarray(scaled.reshape(k // 512, 128, 4, n).transpose(0, 1, 3, 2)).astype(ml_dtypes.float8_e4m3fn).view(np.uint8)
    return words, np.ascontiguousarray(byte.astype(np.uint8).reshape(k // 512, 16, n))


def unpack_weight(words, scales):
    g, p, n, _ = words.shape
    vals = np.ascontiguousarray(words).view(ml_dtypes.float8_e4m3fn).astype(np.float64) * np.repeat(np.exp2(scales.astype(np.float64) - 127.0), 8, axis=1)[..., None]
    return vals.transpose(0, 1, 3, 2).reshape(g * 512, n)


K, T, S, N = 512, 2048, 1024, 128


def setup_inputs():
    n = np.random.standard_normal
    s = mx_kscale(K)[:, None]
    w1, w2 = n((2, K, N)) / np.sqrt(2 * K) / s[None]
    p1, p2 = pack_weight(w1), pack_weight(w2)
    return {
        "xT": (n((K, S)) * s).astype(np.float32),
        "sT": (n((K, T)) * s).astype(np.float32),
        "w1_words": p1[0],
        "w1_scales": p1[1],
        "w2_words": p2[0],
        "w2_scales": p2[1],
        "b": (0.3 * n((N, 1))).astype(np.float32),
        "offs": striped(np.random.permutation(T)[:S]),
    }


def reference(xT, sT, w1_words, w1_scales, w2_words, w2_scales, b, offs):
    y = unpack_weight(w1_words, w1_scales).T @ mxq(f64(xT), 0, "e4m3") + unpack_weight(w2_words, w2_scales).T @ mxq(f64(sT)[:, unstriped(offs)], 0, "e4m3")
    return y + f64(b)

@@ -1,0 +1,165 @@
+from contextlib import ExitStack
+
+import concourse.mybir as mybir
+
+K, T, S, N = 512, 2048, 1024, 128
+FLOPS = 2 * 2 * K * S * N
+
+F32 = mybir.dt.float32
+BF16 = mybir.dt.bfloat16
+I32 = mybir.dt.int32
+U32 = mybir.dt.uint32
+U16 = mybir.dt.uint16
+U8 = mybir.dt.uint8
+FP8X4 = mybir.dt.float8_e4m3fn_x4
+COPY = mybir.ActivationFunctionType.Copy
+IDENTITY = mybir.ActivationFunctionType.Identity
+
+P = 128
+SLICE = 256
+SLICES = S // SLICE
+HALF = S // 2
+
+
+def tile_picked_recall_bias_e_kernel(tc, xT, sT, w1_words, w1_scales, w2_words, w2_scales, b, offs, out):
+    nc = tc.nc
+    with ExitStack() as ctx:
+        keep = ctx.enter_context(tc.tile_pool(name="keep", bufs=1))
+        psum = ctx.enter_context(tc.psum_pool(name="psum", bufs=1))
+
+        offsets = keep.tile([P, S // 16], U16, name="offsets")
+        w1_codes = keep.tile([P, N], U32, name="w1_codes", align_bytes=64)
+        w2_codes = keep.tile([P, N], U32, name="w2_codes", align_bytes=64)
+        w_bytes = keep.tile([P, 2 * N], U8, name="w_bytes", align_bytes=64)
+        bias = keep.tile([P, 1], F32, name="bias")
+        warm = keep.tile([P, 1], F32, name="warm")
+
+        s_rows = sT.rearrange("(p t) w -> p t w", t=4)
+        x_rows = xT.rearrange("(p t) w -> p t w", t=4)
+        s_chunks = [(0, 0, 1024), (0, 1024, 2048), (1, 0, 1024), (1, 1024, 1536), (1, 1536, 2048)]
+        x_chunks = [(lo, lo + SLICE) for lo in (0, 512, 256, 768)]
+        s_raw = [keep.tile([P, 2, hi - lo], F32, name=f"s_raw{i}") for i, (u, lo, hi) in enumerate(s_chunks)]
+        x_raw = [keep.tile([P, 4, hi - lo], F32, name=f"x_raw{i}") for i, (lo, hi) in enumerate(x_chunks)]
+
+        def load_s(i):
+            u, lo, hi = s_chunks[i]
+            nc.sync.dma_start(s_raw[i][:], s_rows[:, 2 * u : 2 * u + 2, lo:hi])
+
+        def load_codes(side):
+            codes, words = ((w1_codes, w1_words), (w2_codes, w2_words))[side]
+            nc.sync.dma_start(codes[:].bitcast(I32), words[0].rearrange("p n t -> p (n t)").bitcast(I32))
+
+        nc.vector.memset(w_bytes[:].bitcast(I32), 0)
+        nc.vector.memset(warm[:], 0.0)
+        nc.scalar.activation(warm[:], warm[:], IDENTITY)
+
+        def load_scales(side):
+            scales = (w1_scales, w2_scales)[side]
+            for quad in range(4):
+                nc.sync.dma_start(
+                    w_bytes[32 * quad : 32 * quad + 4, side * N : (side + 1) * N].bitcast(I32),
+                    scales[0, 4 * quad : 4 * quad + 4, :].bitcast(I32),
+                )
+
+        load_s(0)
+        nc.sync.dma_start(offsets[:], offs)
+        load_scales(1)
+        load_s(1)
+        nc.sync.dma_start(bias[:], b)
+        load_s(2)
+        load_scales(0)
+        load_s(3)
+        load_codes(1)
+        load_s(4)
+        load_codes(0)
+        for i, (lo, hi) in enumerate(x_chunks):
+            nc.sync.dma_start(x_raw[i][:], x_rows[:, :, lo:hi])
+
+        pairs = [keep.tile([P, 2 * T], BF16, name=f"pairs{u}", align_bytes=64) for u in range(2)]
+        picked = [keep.tile([P, HALF, 4], BF16, name=f"picked{h}", align_bytes=64) for h in range(2)]
+        s_codes = [keep.tile([P, HALF], U32, name=f"s_codes{h}", align_bytes=64) for h in range(2)]
+        s_bytes = [keep.tile([P, HALF], U8, name=f"s_bytes{h}", align_bytes=64) for h in range(2)]
+        x_grouped = [keep.tile([P, SLICE, 4], BF16, name=f"x_grouped{j}", align_bytes=64) for j in range(SLICES)]
+        x_codes = [keep.tile([P, SLICE], U32, name=f"x_codes{j}", align_bytes=64) for j in range(SLICES)]
+        x_bytes = [keep.tile([P, SLICE], U8, name=f"x_bytes{j}", align_bytes=64) for j in range(SLICES)]
+        result = [keep.tile([P, HALF], F32, name=f"result{h}", align_bytes=64) for h in range(2)]
+        banks = [psum.tile([P, HALF], F32, name=f"bank{h}") for h in range(2)]
+
+        def move(engine, dst, src):
+            if engine == "v":
+                nc.vector.tensor_copy(dst, src)
+            else:
+                nc.scalar.activation(dst, src, COPY)
+
+        def cast_s(engine, i, a, z):
+            u, lo, hi = s_chunks[i]
+            dst = pairs[u][:].rearrange("p (w e) -> p w e", e=2)[:, lo + a : lo + z, :]
+            move(engine, dst, s_raw[i][:, :, a:z].rearrange("p e w -> p w e"))
+
+        def cast_x(engine, j, a, z):
+            move(engine, x_grouped[j][:, a:z, :], x_raw[j][:, :, a:z].rearrange("p t w -> p w t"))
+
+        def gather(u, h):
+            nc.vector.tensor_copy(
+                picked[h][:].bitcast(U32)[:, :, u],
+                pairs[u][:].bitcast(U32).indirect(offsets[:, h * HALF // 16 : (h + 1) * HALF // 16]),
+            )
+
+        def quantize(grouped, codes, scale_bytes):
+            nc.vector.quantize_mx(
+                out=codes[:].bitcast(FP8X4),
+                scales=scale_bytes[:],
+                in_=grouped[:].rearrange("p w t -> p (w t)"),
+            )
+
+        def finish_x(j):
+            h, i = j % 2, j // 2
+            cols = slice(i * SLICE, (i + 1) * SLICE)
+            quantize(x_grouped[j], x_codes[j], x_bytes[j])
+            nc.tensor.matmul_mx(
+                out=banks[h][:, cols],
+                lhsT=w2_codes[:].bitcast(FP8X4),
+                lhsT_scale=w_bytes[:, N : 2 * N],
+                rhs=s_codes[h][:, cols].bitcast(FP8X4),
+                rhs_scale=s_bytes[h][:, cols],
+                start=True,
+                stop=False,
+            )
+            nc.tensor.matmul_mx(
+                out=banks[h][:, cols],
+                lhsT=w1_codes[:].bitcast(FP8X4),
+                lhsT_scale=w_bytes[:, 0:N],
+                rhs=x_codes[j][:].bitcast(FP8X4),
+                rhs_scale=x_bytes[j][:],
+                start=False,
+                stop=True,
+            )
+
+        def store(h):
+            nc.scalar.activation(result[h][:], banks[h][:], IDENTITY, bias=bias[:])
+            nc.sync.dma_start(out[:, h * HALF : (h + 1) * HALF], result[h][:])
+
+        cast_s("s", 0, 0, 512)
+        cast_s("v", 0, 512, 1024)
+        cast_s("s", 1, 0, 352)
+        cast_s("v", 1, 352, 1024)
+        gather(0, 0)
+        gather(0, 1)
+        cast_s("s", 2, 0, 512)
+        cast_s("s", 2, 512, 1024)
+        cast_s("v", 3, 0, 512)
+        cast_s("s", 4, 0, 176)
+        cast_s("v", 4, 176, 512)
+        gather(1, 0)
+        gather(1, 1)
+        for j in range(3):
+            cast_x("s", j, 0, 256)
+        quantize(picked[0], s_codes[0], s_bytes[0])
+        finish_x(0)
+        quantize(picked[1], s_codes[1], s_bytes[1])
+        finish_x(1)
+        finish_x(2)
+        store(0)
+        cast_x("v", 3, 0, 256)
+        finish_x(3)
+        store(1)

@@ -36,8 +36,8 @@ def tile_picked_recall_bias_e_kernel(tc, xT, sT, w1_words, w1_scales, w2_words, 
 
         s_rows = sT.rearrange("(p t) w -> p t w", t=4)
         x_rows = xT.rearrange("(p t) w -> p t w", t=4)
-        s_chunks = [(0, 0, 1024), (0, 1024, 2048), (1, 0, 1024), (1, 1024, 1536), (1, 1536, 2048)]
-        x_chunks = [(lo, lo + SLICE) for lo in (0, 512, 256, 768)]
+        s_chunks = [(0, 0, 1024), (0, 1024, 2048), (1, 0, 1024), (1, 1024, 1664), (1, 1664, 2048)]
+        x_chunks = [(lo, lo + SLICE) for lo in range(0, S, SLICE)]
         s_raw = [keep.tile([P, 2, hi - lo], F32, name=f"s_raw{i}") for i, (u, lo, hi) in enumerate(s_chunks)]
         x_raw = [keep.tile([P, 4, hi - lo], F32, name=f"x_raw{i}") for i, (lo, hi) in enumerate(x_chunks)]
 
@@ -53,27 +53,31 @@ def tile_picked_recall_bias_e_kernel(tc, xT, sT, w1_words, w1_scales, w2_words, 
         nc.vector.memset(warm[:], 0.0)
         nc.scalar.activation(warm[:], warm[:], IDENTITY)
 
-        def load_scales(side):
+        def load_scales(side, quad):
             scales = (w1_scales, w2_scales)[side]
-            for quad in range(4):
-                nc.sync.dma_start(
-                    w_bytes[32 * quad : 32 * quad + 4, side * N : (side + 1) * N].bitcast(I32),
-                    scales[0, 4 * quad : 4 * quad + 4, :].bitcast(I32),
-                )
+            nc.gpsimd.dma_start(
+                w_bytes[32 * quad : 32 * quad + 4, side * N : (side + 1) * N].bitcast(I32),
+                scales[0, 4 * quad : 4 * quad + 4, :].bitcast(I32),
+            )
 
+        def load_x(j):
+            lo, hi = x_chunks[j]
+            nc.sync.dma_start(x_raw[j][:], x_rows[:, :, lo:hi])
+
+        for side in (1, 0):
+            for quad in range(4):
+                load_scales(side, quad)
         load_s(0)
         nc.sync.dma_start(offsets[:], offs)
-        load_scales(1)
-        load_s(1)
-        nc.sync.dma_start(bias[:], b)
-        load_s(2)
-        load_scales(0)
-        load_s(3)
+        for i in range(1, 5):
+            load_s(i)
+        load_x(0)
         load_codes(1)
-        load_s(4)
+        load_x(1)
         load_codes(0)
-        for i, (lo, hi) in enumerate(x_chunks):
-            nc.sync.dma_start(x_raw[i][:], x_rows[:, :, lo:hi])
+        load_x(2)
+        load_x(3)
+        nc.sync.dma_start(bias[:], b)
 
         pairs = [keep.tile([P, 2 * T], BF16, name=f"pairs{u}", align_bytes=64) for u in range(2)]
         picked = [keep.tile([P, HALF, 4], BF16, name=f"picked{h}", align_bytes=64) for h in range(2)]
@@ -82,8 +86,9 @@ def tile_picked_recall_bias_e_kernel(tc, xT, sT, w1_words, w1_scales, w2_words, 
         x_grouped = [keep.tile([P, SLICE, 4], BF16, name=f"x_grouped{j}", align_bytes=64) for j in range(SLICES)]
         x_codes = [keep.tile([P, SLICE], U32, name=f"x_codes{j}", align_bytes=64) for j in range(SLICES)]
         x_bytes = [keep.tile([P, SLICE], U8, name=f"x_bytes{j}", align_bytes=64) for j in range(SLICES)]
-        result = [keep.tile([P, HALF], F32, name=f"result{h}", align_bytes=64) for h in range(2)]
-        banks = [psum.tile([P, HALF], F32, name=f"bank{h}") for h in range(2)]
+        spans = [(0, 256), (256, 512), (512, 768), (768, 896), (896, 1024)]
+        banks = [psum.tile([P, hi - lo], F32, name=f"bank{i}") for i, (lo, hi) in enumerate(spans)]
+        result = x_raw[SLICES - 1][:].rearrange("p t w -> p (t w)")
 
         def move(engine, dst, src):
             if engine == "v":
@@ -97,7 +102,11 @@ def tile_picked_recall_bias_e_kernel(tc, xT, sT, w1_words, w1_scales, w2_words, 
             move(engine, dst, s_raw[i][:, :, a:z].rearrange("p e w -> p w e"))
 
         def cast_x(engine, j, a, z):
-            move(engine, x_grouped[j][:, a:z, :], x_raw[j][:, :, a:z].rearrange("p t w -> p w t"))
+            move(
+                engine,
+                x_grouped[j][:, a:z, :].rearrange("p (c i) t -> p c t i", i=4),
+                x_raw[j][:, :, a:z].rearrange("p t (c i) -> p c t i", i=4),
+            )
 
         def gather(u, h):
             nc.vector.tensor_copy(
@@ -112,12 +121,12 @@ def tile_picked_recall_bias_e_kernel(tc, xT, sT, w1_words, w1_scales, w2_words, 
                 in_=grouped[:].rearrange("p w t -> p (w t)"),
             )
 
-        def finish_x(j):
-            h, i = j % 2, j // 2
-            cols = slice(i * SLICE, (i + 1) * SLICE)
-            quantize(x_grouped[j], x_codes[j], x_bytes[j])
+        def s_pass(i):
+            lo, hi = spans[i]
+            h = lo // HALF
+            cols = slice(lo - h * HALF, hi - h * HALF)
             nc.tensor.matmul_mx(
-                out=banks[h][:, cols],
+                out=banks[i][:],
                 lhsT=w2_codes[:].bitcast(FP8X4),
                 lhsT_scale=w_bytes[:, N : 2 * N],
                 rhs=s_codes[h][:, cols].bitcast(FP8X4),
@@ -125,19 +134,30 @@ def tile_picked_recall_bias_e_kernel(tc, xT, sT, w1_words, w1_scales, w2_words, 
                 start=True,
                 stop=False,
             )
+
+        def x_pass(i):
+            lo, hi = spans[i]
+            j = lo // SLICE
+            cols = slice(lo - j * SLICE, hi - j * SLICE)
             nc.tensor.matmul_mx(
-                out=banks[h][:, cols],
+                out=banks[i][:],
                 lhsT=w1_codes[:].bitcast(FP8X4),
                 lhsT_scale=w_bytes[:, 0:N],
-                rhs=x_codes[j][:].bitcast(FP8X4),
-                rhs_scale=x_bytes[j][:],
+                rhs=x_codes[j][:, cols].bitcast(FP8X4),
+                rhs_scale=x_bytes[j][:, cols],
                 start=False,
                 stop=True,
             )
 
-        def store(h):
-            nc.scalar.activation(result[h][:], banks[h][:], IDENTITY, bias=bias[:])
-            nc.sync.dma_start(out[:, h * HALF : (h + 1) * HALF], result[h][:])
+        def evict(engine, i):
+            lo, hi = spans[i]
+            if engine == "v":
+                nc.vector.tensor_scalar_add(result[:, lo:hi], banks[i][:], bias[:])
+            else:
+                nc.scalar.activation(result[:, lo:hi], banks[i][:], IDENTITY, bias=bias[:])
+
+        def store(lo, hi):
+            nc.sync.dma_start(out[:, lo:hi], result[:, lo:hi])
 
         cast_s("s", 0, 0, 512)
         cast_s("v", 0, 512, 1024)
@@ -147,19 +167,35 @@ def tile_picked_recall_bias_e_kernel(tc, xT, sT, w1_words, w1_scales, w2_words, 
         gather(0, 1)
         cast_s("s", 2, 0, 512)
         cast_s("s", 2, 512, 1024)
-        cast_s("v", 3, 0, 512)
-        cast_s("s", 4, 0, 176)
-        cast_s("v", 4, 176, 512)
+        cast_s("v", 3, 0, 640)
+        cast_s("s", 4, 0, 128)
+        cast_s("v", 4, 128, 384)
         gather(1, 0)
         gather(1, 1)
         for j in range(3):
             cast_x("s", j, 0, 256)
         quantize(picked[0], s_codes[0], s_bytes[0])
-        finish_x(0)
+        s_pass(0)
+        s_pass(1)
         quantize(picked[1], s_codes[1], s_bytes[1])
-        finish_x(1)
-        finish_x(2)
-        store(0)
-        cast_x("v", 3, 0, 256)
-        finish_x(3)
-        store(1)
+        s_pass(2)
+        s_pass(3)
+        s_pass(4)
+        for j in range(2):
+            quantize(x_grouped[j], x_codes[j], x_bytes[j])
+            x_pass(j)
+        cast_x("s", 3, 0, 128)
+        cast_x("v", 3, 128, 256)
+        quantize(x_grouped[2], x_codes[2], x_bytes[2])
+        x_pass(2)
+        quantize(x_grouped[3], x_codes[3], x_bytes[3])
+        evict("s", 0)
+        evict("s", 1)
+        store(0, 512)
+        evict("s", 2)
+        store(512, 768)
+        x_pass(3)
+        x_pass(4)
+        evict("s", 3)
+        evict("v", 4)
+        store(768, 1024)

@@ -55,7 +55,7 @@ def tile_picked_recall_bias_e_kernel(tc, xT, sT, w1_words, w1_scales, w2_words, 
 
         def load_scales(side, quad):
             scales = (w1_scales, w2_scales)[side]
-            nc.gpsimd.dma_start(
+            nc.sync.dma_start(
                 w_bytes[32 * quad : 32 * quad + 4, side * N : (side + 1) * N].bitcast(I32),
                 scales[0, 4 * quad : 4 * quad + 4, :].bitcast(I32),
             )
@@ -64,18 +64,23 @@ def tile_picked_recall_bias_e_kernel(tc, xT, sT, w1_words, w1_scales, w2_words, 
             lo, hi = x_chunks[j]
             nc.sync.dma_start(x_raw[j][:], x_rows[:, :, lo:hi])
 
-        for side in (1, 0):
-            for quad in range(4):
-                load_scales(side, quad)
         load_s(0)
         nc.sync.dma_start(offsets[:], offs)
-        for i in range(1, 5):
-            load_s(i)
+        load_s(1)
+        for quad in range(4):
+            load_scales(1, quad)
+        load_s(2)
+        for quad in range(2):
+            load_scales(0, quad)
+        load_s(3)
+        for quad in range(2, 4):
+            load_scales(0, quad)
+        load_s(4)
         load_x(0)
-        load_codes(1)
         load_x(1)
-        load_codes(0)
+        load_codes(1)
         load_x(2)
+        load_codes(0)
         load_x(3)
         nc.sync.dma_start(bias[:], b)
 
@@ -190,8 +195,9 @@ def tile_picked_recall_bias_e_kernel(tc, xT, sT, w1_words, w1_scales, w2_words, 
         x_pass(2)
         quantize(x_grouped[3], x_codes[3], x_bytes[3])
         evict("s", 0)
+        store(0, 256)
         evict("s", 1)
-        store(0, 512)
+        store(256, 512)
         evict("s", 2)
         store(512, 768)
         x_pass(3)

@@ -36,7 +36,7 @@ def tile_picked_recall_bias_e_kernel(tc, xT, sT, w1_words, w1_scales, w2_words, 
 
         s_rows = sT.rearrange("(p t) w -> p t w", t=4)
         x_rows = xT.rearrange("(p t) w -> p t w", t=4)
-        s_chunks = [(0, 0, 1024), (0, 1024, 2048), (1, 0, 1024), (1, 1024, 1664), (1, 1664, 2048)]
+        s_chunks = [(0, 0, 1024), (0, 1024, 2048)] + [(1, lo, lo + 512) for lo in range(0, T, 512)]
         x_chunks = [(lo, lo + SLICE) for lo in range(0, S, SLICE)]
         s_raw = [keep.tile([P, 2, hi - lo], F32, name=f"s_raw{i}") for i, (u, lo, hi) in enumerate(s_chunks)]
         x_raw = [keep.tile([P, 4, hi - lo], F32, name=f"x_raw{i}") for i, (lo, hi) in enumerate(x_chunks)]
@@ -66,17 +66,16 @@ def tile_picked_recall_bias_e_kernel(tc, xT, sT, w1_words, w1_scales, w2_words, 
 
         load_s(0)
         nc.sync.dma_start(offsets[:], offs)
-        load_s(1)
+        for i in range(1, 4):
+            load_s(i)
         for quad in range(4):
             load_scales(1, quad)
-        load_s(2)
-        for quad in range(2):
-            load_scales(0, quad)
-        load_s(3)
-        for quad in range(2, 4):
-            load_scales(0, quad)
+        load_scales(0, 0)
         load_s(4)
+        load_s(5)
         load_x(0)
+        for quad in range(1, 4):
+            load_scales(0, quad)
         load_x(1)
         load_codes(1)
         load_x(2)
@@ -170,14 +169,13 @@ def tile_picked_recall_bias_e_kernel(tc, xT, sT, w1_words, w1_scales, w2_words, 
         cast_s("v", 1, 352, 1024)
         gather(0, 0)
         gather(0, 1)
-        cast_s("s", 2, 0, 512)
-        cast_s("s", 2, 512, 1024)
-        cast_s("v", 3, 0, 640)
-        cast_s("s", 4, 0, 128)
-        cast_s("v", 4, 128, 384)
+        for i in range(2, 5):
+            cast_s("s", i, 0, 512)
+        cast_s("s", 5, 0, 160)
+        cast_s("v", 5, 160, 512)
         gather(1, 0)
         gather(1, 1)
-        for j in range(3):
+        for j in range(SLICES):
             cast_x("s", j, 0, 256)
         quantize(picked[0], s_codes[0], s_bytes[0])
         s_pass(0)
@@ -186,13 +184,9 @@ def tile_picked_recall_bias_e_kernel(tc, xT, sT, w1_words, w1_scales, w2_words, 
         s_pass(2)
         s_pass(3)
         s_pass(4)
-        for j in range(2):
+        for j in range(3):
             quantize(x_grouped[j], x_codes[j], x_bytes[j])
             x_pass(j)
-        cast_x("s", 3, 0, 128)
-        cast_x("v", 3, 128, 256)
-        quantize(x_grouped[2], x_codes[2], x_bytes[2])
-        x_pass(2)
         quantize(x_grouped[3], x_codes[3], x_bytes[3])
         evict("s", 0)
         store(0, 256)

@@ -36,7 +36,7 @@ def tile_picked_recall_bias_e_kernel(tc, xT, sT, w1_words, w1_scales, w2_words, 
 
         s_rows = sT.rearrange("(p t) w -> p t w", t=4)
         x_rows = xT.rearrange("(p t) w -> p t w", t=4)
-        s_chunks = [(0, 0, 1024), (0, 1024, 2048)] + [(1, lo, lo + 512) for lo in range(0, T, 512)]
+        s_chunks = [(0, 0, 1536), (0, 1536, 2048), (1, 0, 512), (1, 512, 1152), (1, 1152, 1792), (1, 1792, 2048)]
         x_chunks = [(lo, lo + SLICE) for lo in range(0, S, SLICE)]
         s_raw = [keep.tile([P, 2, hi - lo], F32, name=f"s_raw{i}") for i, (u, lo, hi) in enumerate(s_chunks)]
         x_raw = [keep.tile([P, 4, hi - lo], F32, name=f"x_raw{i}") for i, (lo, hi) in enumerate(x_chunks)]
@@ -118,11 +118,11 @@ def tile_picked_recall_bias_e_kernel(tc, xT, sT, w1_words, w1_scales, w2_words, 
                 pairs[u][:].bitcast(U32).indirect(offsets[:, h * HALF // 16 : (h + 1) * HALF // 16]),
             )
 
-        def quantize(grouped, codes, scale_bytes):
+        def quantize(grouped, codes, scale_bytes, cols=slice(None)):
             nc.vector.quantize_mx(
-                out=codes[:].bitcast(FP8X4),
-                scales=scale_bytes[:],
-                in_=grouped[:].rearrange("p w t -> p (w t)"),
+                out=codes[:, cols].bitcast(FP8X4),
+                scales=scale_bytes[:, cols],
+                in_=grouped[:, cols, :].rearrange("p w t -> p (w t)"),
             )
 
         def s_pass(i):
@@ -160,23 +160,26 @@ def tile_picked_recall_bias_e_kernel(tc, xT, sT, w1_words, w1_scales, w2_words, 
             else:
                 nc.scalar.activation(result[:, lo:hi], banks[i][:], IDENTITY, bias=bias[:])
 
-        def store(lo, hi):
-            nc.sync.dma_start(out[:, lo:hi], result[:, lo:hi])
+        def store(lo, hi, queue=nc.sync):
+            queue.dma_start(out[:, lo:hi], result[:, lo:hi])
 
         cast_s("s", 0, 0, 512)
-        cast_s("v", 0, 512, 1024)
-        cast_s("s", 1, 0, 352)
-        cast_s("v", 1, 352, 1024)
+        cast_s("v", 0, 512, 1536)
+        cast_s("s", 1, 0, 160)
+        cast_s("v", 1, 160, 512)
         gather(0, 0)
         gather(0, 1)
-        for i in range(2, 5):
-            cast_s("s", i, 0, 512)
-        cast_s("s", 5, 0, 160)
-        cast_s("v", 5, 160, 512)
+        cast_s("s", 2, 0, 512)
+        cast_s("s", 3, 0, 640)
+        cast_s("s", 4, 0, 320)
+        cast_s("v", 4, 320, 640)
+        cast_s("s", 5, 0, 80)
+        cast_s("v", 5, 80, 256)
         gather(1, 0)
         gather(1, 1)
-        for j in range(SLICES):
+        for j in range(3):
             cast_x("s", j, 0, 256)
+        cast_x("s", 3, 0, 192)
         quantize(picked[0], s_codes[0], s_bytes[0])
         s_pass(0)
         s_pass(1)
@@ -184,18 +187,22 @@ def tile_picked_recall_bias_e_kernel(tc, xT, sT, w1_words, w1_scales, w2_words, 
         s_pass(2)
         s_pass(3)
         s_pass(4)
-        for j in range(3):
+        for j in range(2):
             quantize(x_grouped[j], x_codes[j], x_bytes[j])
             x_pass(j)
+        cast_x("v", 3, 192, 256)
+        quantize(x_grouped[2], x_codes[2], x_bytes[2])
+        x_pass(2)
         quantize(x_grouped[3], x_codes[3], x_bytes[3])
         evict("s", 0)
         store(0, 256)
         evict("s", 1)
         store(256, 512)
-        evict("s", 2)
+        evict("v", 2)
         store(512, 768)
         x_pass(3)
         x_pass(4)
         evict("s", 3)
+        store(768, 896, nc.scalar)
         evict("v", 4)
-        store(768, 1024)
+        store(896, 1024)

@@ -32,11 +32,10 @@ def tile_picked_recall_bias_e_kernel(tc, xT, sT, w1_words, w1_scales, w2_words, 
         w2_codes = keep.tile([P, N], U32, name="w2_codes", align_bytes=64)
         w_bytes = keep.tile([P, 2 * N], U8, name="w_bytes", align_bytes=64)
         bias = keep.tile([P, 1], F32, name="bias")
-        warm = keep.tile([P, 1], F32, name="warm")
 
         s_rows = sT.rearrange("(p t) w -> p t w", t=4)
         x_rows = xT.rearrange("(p t) w -> p t w", t=4)
-        s_chunks = [(0, 0, 1536), (0, 1536, 2048), (1, 0, 512), (1, 512, 1152), (1, 1152, 1792), (1, 1792, 2048)]
+        s_chunks = [(0, 0, 1024), (0, 1024, 2048), (1, 0, 512), (1, 512, 1024), (1, 1024, 1536), (1, 1536, 1792), (1, 1792, 2048)]
         x_chunks = [(lo, lo + SLICE) for lo in range(0, S, SLICE)]
         s_raw = [keep.tile([P, 2, hi - lo], F32, name=f"s_raw{i}") for i, (u, lo, hi) in enumerate(s_chunks)]
         x_raw = [keep.tile([P, 4, hi - lo], F32, name=f"x_raw{i}") for i, (lo, hi) in enumerate(x_chunks)]
@@ -50,8 +49,6 @@ def tile_picked_recall_bias_e_kernel(tc, xT, sT, w1_words, w1_scales, w2_words, 
             nc.sync.dma_start(codes[:].bitcast(I32), words[0].rearrange("p n t -> p (n t)").bitcast(I32))
 
         nc.vector.memset(w_bytes[:].bitcast(I32), 0)
-        nc.vector.memset(warm[:], 0.0)
-        nc.scalar.activation(warm[:], warm[:], IDENTITY)
 
         def load_scales(side, quad):
             scales = (w1_scales, w2_scales)[side]
@@ -64,24 +61,22 @@ def tile_picked_recall_bias_e_kernel(tc, xT, sT, w1_words, w1_scales, w2_words, 
             lo, hi = x_chunks[j]
             nc.sync.dma_start(x_raw[j][:], x_rows[:, :, lo:hi])
 
+        def load_weights(side):
+            load_codes(side)
+            for quad in range(4):
+                load_scales(side, quad)
+
         load_s(0)
         nc.sync.dma_start(offsets[:], offs)
-        for i in range(1, 4):
+        for i in range(1, len(s_chunks)):
             load_s(i)
-        for quad in range(4):
-            load_scales(1, quad)
-        load_scales(0, 0)
-        load_s(4)
-        load_s(5)
         load_x(0)
-        for quad in range(1, 4):
-            load_scales(0, quad)
         load_x(1)
-        load_codes(1)
+        load_weights(1)
         load_x(2)
-        load_codes(0)
         load_x(3)
         nc.sync.dma_start(bias[:], b)
+        load_weights(0)
 
         pairs = [keep.tile([P, 2 * T], BF16, name=f"pairs{u}", align_bytes=64) for u in range(2)]
         picked = [keep.tile([P, HALF, 4], BF16, name=f"picked{h}", align_bytes=64) for h in range(2)]
@@ -160,26 +155,24 @@ def tile_picked_recall_bias_e_kernel(tc, xT, sT, w1_words, w1_scales, w2_words, 
             else:
                 nc.scalar.activation(result[:, lo:hi], banks[i][:], IDENTITY, bias=bias[:])
 
-        def store(lo, hi, queue=nc.sync):
-            queue.dma_start(out[:, lo:hi], result[:, lo:hi])
+        def store(lo, hi):
+            nc.sync.dma_start(out[:, lo:hi], result[:, lo:hi])
 
-        cast_s("s", 0, 0, 512)
-        cast_s("v", 0, 512, 1536)
-        cast_s("s", 1, 0, 160)
-        cast_s("v", 1, 160, 512)
+        cast_s("s", 0, 0, 256)
+        cast_s("v", 0, 256, 1024)
+        cast_s("s", 1, 0, 352)
+        cast_s("v", 1, 352, 1024)
         gather(0, 0)
         gather(0, 1)
-        cast_s("s", 2, 0, 512)
-        cast_s("s", 3, 0, 640)
-        cast_s("s", 4, 0, 320)
-        cast_s("v", 4, 320, 640)
-        cast_s("s", 5, 0, 80)
-        cast_s("v", 5, 80, 256)
+        for i in range(2, 5):
+            cast_s("s", i, 0, 512)
+        cast_s("v", 5, 0, 256)
+        cast_s("s", 6, 0, 96)
+        cast_s("v", 6, 96, 256)
         gather(1, 0)
         gather(1, 1)
-        for j in range(3):
+        for j in range(SLICES):
             cast_x("s", j, 0, 256)
-        cast_x("s", 3, 0, 192)
         quantize(picked[0], s_codes[0], s_bytes[0])
         s_pass(0)
         s_pass(1)
@@ -187,13 +180,11 @@ def tile_picked_recall_bias_e_kernel(tc, xT, sT, w1_words, w1_scales, w2_words, 
         s_pass(2)
         s_pass(3)
         s_pass(4)
-        for j in range(2):
+        for j in range(3):
             quantize(x_grouped[j], x_codes[j], x_bytes[j])
             x_pass(j)
-        cast_x("v", 3, 192, 256)
-        quantize(x_grouped[2], x_codes[2], x_bytes[2])
-        x_pass(2)
-        quantize(x_grouped[3], x_codes[3], x_bytes[3])
+        quantize(x_grouped[3], x_codes[3], x_bytes[3], slice(0, 128))
+        quantize(x_grouped[3], x_codes[3], x_bytes[3], slice(128, 256))
         evict("s", 0)
         store(0, 256)
         evict("s", 1)
@@ -203,6 +194,5 @@ def tile_picked_recall_bias_e_kernel(tc, xT, sT, w1_words, w1_scales, w2_words, 
         x_pass(3)
         x_pass(4)
         evict("s", 3)
-        store(768, 896, nc.scalar)
         evict("v", 4)
-        store(896, 1024)
+        store(768, 1024)

@@ -16,9 +16,9 @@ COPY = mybir.ActivationFunctionType.Copy
 IDENTITY = mybir.ActivationFunctionType.Identity
 
 P = 128
-SLICE = 256
-SLICES = S // SLICE
 HALF = S // 2
+MULT = mybir.AluOpType.mult
+ADD = mybir.AluOpType.add
 
 
 def tile_picked_recall_bias_e_kernel(tc, xT, sT, w1_words, w1_scales, w2_words, w2_scales, b, offs, out):
@@ -36,9 +36,12 @@ def tile_picked_recall_bias_e_kernel(tc, xT, sT, w1_words, w1_scales, w2_words, 
         s_rows = sT.rearrange("(p t) w -> p t w", t=4)
         x_rows = xT.rearrange("(p t) w -> p t w", t=4)
         s_chunks = [(0, 0, 1024), (0, 1024, 2048), (1, 0, 512), (1, 512, 1024), (1, 1024, 1536), (1, 1536, 1792), (1, 1792, 2048)]
-        x_chunks = [(lo, lo + SLICE) for lo in range(0, S, SLICE)]
+        x_chunks = [(lo, lo + 128) for lo in range(0, S, 128)]
+        spans = [(0, 256), (256, 512), (512, 768), (768, 896), (896, 1024)]
         s_raw = [keep.tile([P, 2, hi - lo], F32, name=f"s_raw{i}") for i, (u, lo, hi) in enumerate(s_chunks)]
-        x_raw = [keep.tile([P, 4, hi - lo], F32, name=f"x_raw{i}") for i, (lo, hi) in enumerate(x_chunks)]
+        whole = keep.tile([P, S], F32, name="whole")
+        x_raw = [keep.tile([P, 4, hi - lo], F32, name=f"x_raw{i}")[:] for i, (lo, hi) in enumerate(x_chunks[:-1])]
+        x_raw.append(whole[:].rearrange("p (t w) -> p t w", t=4)[:, :, 0:128])
 
         def load_s(i):
             u, lo, hi = s_chunks[i]
@@ -50,74 +53,97 @@ def tile_picked_recall_bias_e_kernel(tc, xT, sT, w1_words, w1_scales, w2_words, 
 
         nc.vector.memset(w_bytes[:].bitcast(I32), 0)
 
-        def load_scales(side, quad):
+        def load_scales(side):
             scales = (w1_scales, w2_scales)[side]
-            nc.sync.dma_start(
-                w_bytes[32 * quad : 32 * quad + 4, side * N : (side + 1) * N].bitcast(I32),
-                scales[0, 4 * quad : 4 * quad + 4, :].bitcast(I32),
-            )
+            for quad in range(4):
+                nc.sync.dma_start(
+                    w_bytes[32 * quad : 32 * quad + 4, side * N : (side + 1) * N].bitcast(I32),
+                    scales[0, 4 * quad : 4 * quad + 4, :].bitcast(I32),
+                )
 
         def load_x(j):
             lo, hi = x_chunks[j]
-            nc.sync.dma_start(x_raw[j][:], x_rows[:, :, lo:hi])
-
-        def load_weights(side):
-            load_codes(side)
-            for quad in range(4):
-                load_scales(side, quad)
+            nc.sync.dma_start(x_raw[j], x_rows[:, :, lo:hi])
 
         load_s(0)
         nc.sync.dma_start(offsets[:], offs)
-        for i in range(1, len(s_chunks)):
-            load_s(i)
+        load_scales(1)
+        load_s(1)
+        load_s(2)
+        load_s(3)
+        load_scales(0)
+        load_s(4)
+        load_s(5)
+        load_s(6)
         load_x(0)
         load_x(1)
-        load_weights(1)
         load_x(2)
         load_x(3)
+        load_codes(1)
+        load_x(4)
+        load_codes(0)
+        load_x(5)
         nc.sync.dma_start(bias[:], b)
-        load_weights(0)
+        load_x(6)
+        load_x(7)
 
         pairs = [keep.tile([P, 2 * T], BF16, name=f"pairs{u}", align_bytes=64) for u in range(2)]
-        picked = [keep.tile([P, HALF, 4], BF16, name=f"picked{h}", align_bytes=64) for h in range(2)]
+        flat = keep.tile([P, 2, HALF], U32, name="flat", align_bytes=64)
+        picked = [keep.tile([P, HALF, 2], U32, name=f"picked{h}", align_bytes=64) for h in range(2)]
         s_codes = [keep.tile([P, HALF], U32, name=f"s_codes{h}", align_bytes=64) for h in range(2)]
         s_bytes = [keep.tile([P, HALF], U8, name=f"s_bytes{h}", align_bytes=64) for h in range(2)]
-        x_grouped = [keep.tile([P, SLICE, 4], BF16, name=f"x_grouped{j}", align_bytes=64) for j in range(SLICES)]
-        x_codes = [keep.tile([P, SLICE], U32, name=f"x_codes{j}", align_bytes=64) for j in range(SLICES)]
-        x_bytes = [keep.tile([P, SLICE], U8, name=f"x_bytes{j}", align_bytes=64) for j in range(SLICES)]
-        spans = [(0, 256), (256, 512), (512, 768), (768, 896), (896, 1024)]
+        x_grouped = [keep.tile([P, hi - lo, 4], BF16, name=f"x_grouped{i}", align_bytes=64) for i, (lo, hi) in enumerate(spans)]
+        x_grouped[2] = flat[:, 1, :].bitcast(BF16).rearrange("p (w t) -> p w t", t=4)
+        x_codes = [keep.tile([P, hi - lo], U32, name=f"x_codes{i}", align_bytes=64) for i, (lo, hi) in enumerate(spans)]
+        x_bytes = [keep.tile([P, hi - lo], U8, name=f"x_bytes{i}", align_bytes=64) for i, (lo, hi) in enumerate(spans)]
         banks = [psum.tile([P, hi - lo], F32, name=f"bank{i}") for i, (lo, hi) in enumerate(spans)]
-        result = x_raw[SLICES - 1][:].rearrange("p t w -> p (t w)")
 
-        def move(engine, dst, src):
+        def result(lo, hi):
+            return whole[:, lo:hi]
+
+        def cast_s(engine, i, a, z):
+            u, lo, hi = s_chunks[i]
+            dst = pairs[u][:].rearrange("p (w e) -> p w e", e=2)[:, lo + a : lo + z, :]
+            src = s_raw[i][:, :, a:z].rearrange("p e w -> p w e")
             if engine == "v":
                 nc.vector.tensor_copy(dst, src)
             else:
                 nc.scalar.activation(dst, src, COPY)
 
-        def cast_s(engine, i, a, z):
-            u, lo, hi = s_chunks[i]
-            dst = pairs[u][:].rearrange("p (w e) -> p w e", e=2)[:, lo + a : lo + z, :]
-            move(engine, dst, s_raw[i][:, :, a:z].rearrange("p e w -> p w e"))
-
         def cast_x(engine, j, a, z):
-            move(
-                engine,
-                x_grouped[j][:, a:z, :].rearrange("p (c i) t -> p c t i", i=4),
-                x_raw[j][:, :, a:z].rearrange("p t (c i) -> p c t i", i=4),
-            )
+            lo = x_chunks[j][0]
+            i = max(n for n, span in enumerate(spans) if span[0] <= lo)
+            at = lo - spans[i][0]
+            dst = x_grouped[i][:, at + a : at + z, :]
+            src = x_raw[j][:, :, a:z]
+            if engine == "g":
+                nc.gpsimd.tensor_scalar(dst, src.rearrange("p t c -> p c t"), 1.0, 0.0, MULT, ADD)
+                return
+            dst = dst.rearrange("p (c i) t -> p c t i", i=4)
+            src = src.rearrange("p t (c i) -> p c t i", i=4)
+            if engine == "v":
+                nc.vector.tensor_copy(dst, src)
+            else:
+                nc.scalar.activation(dst, src, COPY)
 
-        def gather(u, h):
-            nc.vector.tensor_copy(
-                picked[h][:].bitcast(U32)[:, :, u],
-                pairs[u][:].bitcast(U32).indirect(offsets[:, h * HALF // 16 : (h + 1) * HALF // 16]),
-            )
+        def gather(dst, u, lo, hi):
+            nc.vector.tensor_copy(dst, pairs[u][:].bitcast(U32).indirect(offsets[:, lo // 16 : hi // 16]))
 
-        def quantize(grouped, codes, scale_bytes, cols=slice(None)):
+        def weave(lo, hi):
+            nc.scalar.copy(picked[1][:, lo:hi, :], flat[:, :, lo:hi].rearrange("p u c -> p c u"))
+
+        def quantize_s(h, lo, hi):
             nc.vector.quantize_mx(
-                out=codes[:, cols].bitcast(FP8X4),
-                scales=scale_bytes[:, cols],
-                in_=grouped[:, cols, :].rearrange("p w t -> p (w t)"),
+                out=s_codes[h][:, lo:hi].bitcast(FP8X4),
+                scales=s_bytes[h][:, lo:hi],
+                in_=picked[h][:, lo:hi, :].rearrange("p w u -> p (w u)").bitcast(BF16),
+            )
+
+        def quantize_x(i):
+            nc.vector.quantize_mx(
+                out=x_codes[i][:].bitcast(FP8X4),
+                scales=x_bytes[i][:],
+                in_=x_grouped[i][:, :, :].rearrange("p w t -> p (w t)"),
             )
 
         def s_pass(i):
@@ -135,15 +161,12 @@ def tile_picked_recall_bias_e_kernel(tc, xT, sT, w1_words, w1_scales, w2_words, 
             )
 
         def x_pass(i):
-            lo, hi = spans[i]
-            j = lo // SLICE
-            cols = slice(lo - j * SLICE, hi - j * SLICE)
             nc.tensor.matmul_mx(
                 out=banks[i][:],
                 lhsT=w1_codes[:].bitcast(FP8X4),
                 lhsT_scale=w_bytes[:, 0:N],
-                rhs=x_codes[j][:, cols].bitcast(FP8X4),
-                rhs_scale=x_bytes[j][:, cols],
+                rhs=x_codes[i][:].bitcast(FP8X4),
+                rhs_scale=x_bytes[i][:],
                 start=False,
                 stop=True,
             )
@@ -151,48 +174,50 @@ def tile_picked_recall_bias_e_kernel(tc, xT, sT, w1_words, w1_scales, w2_words, 
         def evict(engine, i):
             lo, hi = spans[i]
             if engine == "v":
-                nc.vector.tensor_scalar_add(result[:, lo:hi], banks[i][:], bias[:])
+                nc.vector.tensor_scalar_add(result(lo, hi), banks[i][:], bias[:])
             else:
-                nc.scalar.activation(result[:, lo:hi], banks[i][:], IDENTITY, bias=bias[:])
+                nc.scalar.activation(result(lo, hi), banks[i][:], IDENTITY, bias=bias[:])
 
         def store(lo, hi):
-            nc.sync.dma_start(out[:, lo:hi], result[:, lo:hi])
+            nc.sync.dma_start(out[:, lo:hi], result(lo, hi))
 
         cast_s("s", 0, 0, 256)
         cast_s("v", 0, 256, 1024)
         cast_s("s", 1, 0, 352)
         cast_s("v", 1, 352, 1024)
-        gather(0, 0)
-        gather(0, 1)
-        for i in range(2, 5):
-            cast_s("s", i, 0, 512)
+        gather(picked[0][:, :, 0], 0, 0, HALF)
+        gather(flat[:, 0, :], 0, HALF, S)
+        cast_s("s", 2, 0, 512)
+        cast_s("s", 3, 0, 512)
+        cast_s("s", 4, 0, 384)
+        cast_s("v", 4, 384, 512)
         cast_s("v", 5, 0, 256)
         cast_s("s", 6, 0, 96)
         cast_s("v", 6, 96, 256)
-        gather(1, 0)
-        gather(1, 1)
-        for j in range(SLICES):
-            cast_x("s", j, 0, 256)
-        quantize(picked[0], s_codes[0], s_bytes[0])
-        s_pass(0)
-        s_pass(1)
-        quantize(picked[1], s_codes[1], s_bytes[1])
-        s_pass(2)
-        s_pass(3)
-        s_pass(4)
-        for j in range(3):
-            quantize(x_grouped[j], x_codes[j], x_bytes[j])
-            x_pass(j)
-        quantize(x_grouped[3], x_codes[3], x_bytes[3], slice(0, 128))
-        quantize(x_grouped[3], x_codes[3], x_bytes[3], slice(128, 256))
-        evict("s", 0)
-        store(0, 256)
-        evict("s", 1)
-        store(256, 512)
-        evict("v", 2)
-        store(512, 768)
-        x_pass(3)
-        x_pass(4)
+        gather(flat[:, 1, 0:256], 1, 512, 768)
+        gather(flat[:, 1, 256:512], 1, 768, 1024)
+        gather(picked[0][:, 0:256, 1], 1, 0, 256)
+        gather(picked[0][:, 256:512, 1], 1, 256, 512)
+        weave(0, 256)
+        weave(256, 512)
+        for j in range(4):
+            cast_x("g", j, 0, 128)
+        for j in range(4, 8):
+            cast_x("s", j, 0, 128)
+        for i in range(2):
+            quantize_s(0, 256 * i, 256 * i + 256)
+            s_pass(i)
+            quantize_x(i)
+            x_pass(i)
+        quantize_s(1, 0, 512)
+        for i in range(2, 5):
+            s_pass(i)
+        for i in range(2, 5):
+            quantize_x(i)
+            x_pass(i)
+        for i in range(3):
+            evict("s", i)
+            store(*spans[i])
         evict("s", 3)
         evict("v", 4)
         store(768, 1024)

@@ -36,12 +36,13 @@ def tile_picked_recall_bias_e_kernel(tc, xT, sT, w1_words, w1_scales, w2_words, 
         s_rows = sT.rearrange("(p t) w -> p t w", t=4)
         x_rows = xT.rearrange("(p t) w -> p t w", t=4)
         s_chunks = [(0, 0, 1024), (0, 1024, 2048), (1, 0, 512), (1, 512, 1024), (1, 1024, 1536), (1, 1536, 1792), (1, 1792, 2048)]
-        x_chunks = [(lo, lo + 128) for lo in range(0, S, 128)]
-        spans = [(0, 256), (256, 512), (512, 768), (768, 896), (896, 1024)]
+        x_chunks = [(0, 128), (128, 384), (384, 640), (640, 896), (896, 1024)]
+        spans = x_chunks
         s_raw = [keep.tile([P, 2, hi - lo], F32, name=f"s_raw{i}") for i, (u, lo, hi) in enumerate(s_chunks)]
-        whole = keep.tile([P, S], F32, name="whole")
-        x_raw = [keep.tile([P, 4, hi - lo], F32, name=f"x_raw{i}")[:] for i, (lo, hi) in enumerate(x_chunks[:-1])]
-        x_raw.append(whole[:].rearrange("p (t w) -> p t w", t=4)[:, :, 0:128])
+        woven = keep.tile([P, S], F32, name="woven", align_bytes=64)
+        x_raw = [woven[:, 0:512].rearrange("p (t w) -> p t w", t=4)]
+        x_raw.extend(keep.tile([P, 4, hi - lo], F32, name=f"x_raw{lo}")[:] for lo, hi in x_chunks[1:])
+        whole = x_raw[3].rearrange("p t w -> p (t w)")
 
         def load_s(i):
             u, lo, hi = s_chunks[i]
@@ -70,30 +71,26 @@ def tile_picked_recall_bias_e_kernel(tc, xT, sT, w1_words, w1_scales, w2_words, 
         load_scales(1)
         load_s(1)
         load_s(2)
-        load_s(3)
         load_scales(0)
-        load_s(4)
-        load_s(5)
-        load_s(6)
+        for i in range(3, 7):
+            load_s(i)
         load_x(0)
         load_x(1)
         load_x(2)
-        load_x(3)
         load_codes(1)
-        load_x(4)
+        load_x(3)
         load_codes(0)
-        load_x(5)
+        load_x(4)
         nc.sync.dma_start(bias[:], b)
-        load_x(6)
-        load_x(7)
 
         pairs = [keep.tile([P, 2 * T], BF16, name=f"pairs{u}", align_bytes=64) for u in range(2)]
-        flat = keep.tile([P, 2, HALF], U32, name="flat", align_bytes=64)
-        picked = [keep.tile([P, HALF, 2], U32, name=f"picked{h}", align_bytes=64) for h in range(2)]
-        s_codes = [keep.tile([P, HALF], U32, name=f"s_codes{h}", align_bytes=64) for h in range(2)]
-        s_bytes = [keep.tile([P, HALF], U8, name=f"s_bytes{h}", align_bytes=64) for h in range(2)]
+        flat = [keep.tile([P, 2, 256], U32, name=f"flat{q}", align_bytes=64) for q in range(2)]
+        stepped = keep.tile([P, HALF, 2], U32, name="stepped", align_bytes=64)
+        picked = [stepped[:], woven[:].bitcast(U32).rearrange("p (w u) -> p w u", u=2)]
+        s_codes = keep.tile([P, S], U32, name="s_codes", align_bytes=64)
+        s_bytes = keep.tile([P, S], U8, name="s_bytes", align_bytes=64)
         x_grouped = [keep.tile([P, hi - lo, 4], BF16, name=f"x_grouped{i}", align_bytes=64) for i, (lo, hi) in enumerate(spans)]
-        x_grouped[2] = flat[:, 1, :].bitcast(BF16).rearrange("p (w t) -> p w t", t=4)
+        x_grouped[2] = flat[0][:].rearrange("p u c -> p (u c)").bitcast(BF16).rearrange("p (w t) -> p w t", t=4)
         x_codes = [keep.tile([P, hi - lo], U32, name=f"x_codes{i}", align_bytes=64) for i, (lo, hi) in enumerate(spans)]
         x_bytes = [keep.tile([P, hi - lo], U8, name=f"x_bytes{i}", align_bytes=64) for i, (lo, hi) in enumerate(spans)]
         banks = [psum.tile([P, hi - lo], F32, name=f"bank{i}") for i, (lo, hi) in enumerate(spans)]
@@ -130,12 +127,12 @@ def tile_picked_recall_bias_e_kernel(tc, xT, sT, w1_words, w1_scales, w2_words, 
             nc.vector.tensor_copy(dst, pairs[u][:].bitcast(U32).indirect(offsets[:, lo // 16 : hi // 16]))
 
         def weave(lo, hi):
-            nc.scalar.copy(picked[1][:, lo:hi, :], flat[:, :, lo:hi].rearrange("p u c -> p c u"))
+            nc.scalar.copy(picked[1][:, lo:hi, :], flat[lo // 256][:].rearrange("p u c -> p c u"))
 
         def quantize_s(h, lo, hi):
             nc.vector.quantize_mx(
-                out=s_codes[h][:, lo:hi].bitcast(FP8X4),
-                scales=s_bytes[h][:, lo:hi],
+                out=s_codes[:, h * HALF + lo : h * HALF + hi].bitcast(FP8X4),
+                scales=s_bytes[:, h * HALF + lo : h * HALF + hi],
                 in_=picked[h][:, lo:hi, :].rearrange("p w u -> p (w u)").bitcast(BF16),
             )
 
@@ -148,14 +145,12 @@ def tile_picked_recall_bias_e_kernel(tc, xT, sT, w1_words, w1_scales, w2_words, 
 
         def s_pass(i):
             lo, hi = spans[i]
-            h = lo // HALF
-            cols = slice(lo - h * HALF, hi - h * HALF)
             nc.tensor.matmul_mx(
                 out=banks[i][:],
                 lhsT=w2_codes[:].bitcast(FP8X4),
                 lhsT_scale=w_bytes[:, N : 2 * N],
-                rhs=s_codes[h][:, cols].bitcast(FP8X4),
-                rhs_scale=s_bytes[h][:, cols],
+                rhs=s_codes[:, lo:hi].bitcast(FP8X4),
+                rhs_scale=s_bytes[:, lo:hi],
                 start=True,
                 stop=False,
             )
@@ -186,7 +181,8 @@ def tile_picked_recall_bias_e_kernel(tc, xT, sT, w1_words, w1_scales, w2_words, 
         cast_s("s", 1, 0, 352)
         cast_s("v", 1, 352, 1024)
         gather(picked[0][:, :, 0], 0, 0, HALF)
-        gather(flat[:, 0, :], 0, HALF, S)
+        gather(flat[0][:, 0, :], 0, 512, 768)
+        gather(flat[1][:, 0, :], 0, 768, 1024)
         cast_s("s", 2, 0, 512)
         cast_s("s", 3, 0, 512)
         cast_s("s", 4, 0, 384)
@@ -194,30 +190,36 @@ def tile_picked_recall_bias_e_kernel(tc, xT, sT, w1_words, w1_scales, w2_words, 
         cast_s("v", 5, 0, 256)
         cast_s("s", 6, 0, 96)
         cast_s("v", 6, 96, 256)
-        gather(flat[:, 1, 0:256], 1, 512, 768)
-        gather(flat[:, 1, 256:512], 1, 768, 1024)
+        gather(flat[0][:, 1, :], 1, 512, 768)
+        gather(flat[1][:, 1, :], 1, 768, 1024)
         gather(picked[0][:, 0:256, 1], 1, 0, 256)
         gather(picked[0][:, 256:512, 1], 1, 256, 512)
+        cast_x("s", 0, 0, 128)
         weave(0, 256)
         weave(256, 512)
-        for j in range(4):
-            cast_x("g", j, 0, 128)
-        for j in range(4, 8):
-            cast_x("s", j, 0, 128)
-        for i in range(2):
-            quantize_s(0, 256 * i, 256 * i + 256)
-            s_pass(i)
-            quantize_x(i)
-            x_pass(i)
+        cast_x("g", 1, 0, 256)
+        cast_x("s", 2, 0, 256)
+        cast_x("s", 3, 0, 256)
+        quantize_s(0, 0, 256)
+        s_pass(0)
+        quantize_x(0)
+        x_pass(0)
+        quantize_s(0, 256, 512)
+        s_pass(1)
+        quantize_x(1)
+        x_pass(1)
         quantize_s(1, 0, 512)
         for i in range(2, 5):
             s_pass(i)
+        cast_x("v", 4, 0, 128)
         for i in range(2, 5):
             quantize_x(i)
             x_pass(i)
-        for i in range(3):
+        evict("s", 0)
+        evict("s", 1)
+        store(0, 384)
+        for i in range(2, 4):
             evict("s", i)
             store(*spans[i])
-        evict("s", 3)
         evict("v", 4)
-        store(768, 1024)
+        store(*spans[4])

@@ -39,8 +39,8 @@ def tile_picked_recall_bias_e_kernel(tc, xT, sT, w1_words, w1_scales, w2_words, 
         x_chunks = [(0, 128), (128, 384), (384, 640), (640, 896), (896, 1024)]
         spans = x_chunks
         s_raw = [keep.tile([P, 2, hi - lo], F32, name=f"s_raw{i}") for i, (u, lo, hi) in enumerate(s_chunks)]
-        woven = keep.tile([P, S], F32, name="woven", align_bytes=64)
-        x_raw = [woven[:, 0:512].rearrange("p (t w) -> p t w", t=4)]
+        picked = keep.tile([P, 2 * S], F32, name="picked", align_bytes=64)
+        x_raw = [picked[:, 768:1280].rearrange("p (t w) -> p t w", t=4)]
         x_raw.extend(keep.tile([P, 4, hi - lo], F32, name=f"x_raw{lo}")[:] for lo, hi in x_chunks[1:])
         whole = x_raw[3].rearrange("p t w -> p (t w)")
 
@@ -68,31 +68,28 @@ def tile_picked_recall_bias_e_kernel(tc, xT, sT, w1_words, w1_scales, w2_words, 
 
         load_s(0)
         nc.sync.dma_start(offsets[:], offs)
-        load_scales(1)
-        load_s(1)
-        load_s(2)
-        load_scales(0)
-        for i in range(3, 7):
+        nc.sync.dma_start(bias[:], b)
+        for i in range(1, len(s_chunks)):
             load_s(i)
         load_x(0)
         load_x(1)
-        load_x(2)
         load_codes(1)
+        load_scales(1)
+        load_x(2)
         load_x(3)
-        load_codes(0)
         load_x(4)
-        nc.sync.dma_start(bias[:], b)
+        load_codes(0)
+        load_scales(0)
 
         pairs = [keep.tile([P, 2 * T], BF16, name=f"pairs{u}", align_bytes=64) for u in range(2)]
-        flat = [keep.tile([P, 2, 256], U32, name=f"flat{q}", align_bytes=64) for q in range(2)]
-        stepped = keep.tile([P, HALF, 2], U32, name="stepped", align_bytes=64)
-        picked = [stepped[:], woven[:].bitcast(U32).rearrange("p (w u) -> p w u", u=2)]
+        words = picked[:].bitcast(U32).rearrange("p (w u) -> p w u", u=2)
         s_codes = keep.tile([P, S], U32, name="s_codes", align_bytes=64)
         s_bytes = keep.tile([P, S], U8, name="s_bytes", align_bytes=64)
-        x_grouped = [keep.tile([P, hi - lo, 4], BF16, name=f"x_grouped{i}", align_bytes=64) for i, (lo, hi) in enumerate(spans)]
-        x_grouped[2] = flat[0][:].rearrange("p u c -> p (u c)").bitcast(BF16).rearrange("p (w t) -> p w t", t=4)
-        x_codes = [keep.tile([P, hi - lo], U32, name=f"x_codes{i}", align_bytes=64) for i, (lo, hi) in enumerate(spans)]
-        x_bytes = [keep.tile([P, hi - lo], U8, name=f"x_bytes{i}", align_bytes=64) for i, (lo, hi) in enumerate(spans)]
+        x_grouped = keep.tile([P, 4 * S], BF16, name="x_grouped", align_bytes=64)
+        flat_late = keep.tile([P, 2, 256], U32, name="flat_late", align_bytes=64)
+        flat = [x_grouped[:, 4 * 384 : 4 * 640].bitcast(U32).rearrange("p (u c) -> p u c", u=2), flat_late[:]]
+        x_codes = keep.tile([P, S], U32, name="x_codes", align_bytes=64)
+        x_bytes = keep.tile([P, S], U8, name="x_bytes", align_bytes=64)
         banks = [psum.tile([P, hi - lo], F32, name=f"bank{i}") for i, (lo, hi) in enumerate(spans)]
 
         def result(lo, hi):
@@ -109,9 +106,7 @@ def tile_picked_recall_bias_e_kernel(tc, xT, sT, w1_words, w1_scales, w2_words, 
 
         def cast_x(engine, j, a, z):
             lo = x_chunks[j][0]
-            i = max(n for n, span in enumerate(spans) if span[0] <= lo)
-            at = lo - spans[i][0]
-            dst = x_grouped[i][:, at + a : at + z, :]
+            dst = x_grouped[:, 4 * (lo + a) : 4 * (lo + z)].rearrange("p (c t) -> p c t", t=4)
             src = x_raw[j][:, :, a:z]
             if engine == "g":
                 nc.gpsimd.tensor_scalar(dst, src.rearrange("p t c -> p c t"), 1.0, 0.0, MULT, ADD)
@@ -126,21 +121,28 @@ def tile_picked_recall_bias_e_kernel(tc, xT, sT, w1_words, w1_scales, w2_words, 
         def gather(dst, u, lo, hi):
             nc.vector.tensor_copy(dst, pairs[u][:].bitcast(U32).indirect(offsets[:, lo // 16 : hi // 16]))
 
-        def weave(lo, hi):
-            nc.scalar.copy(picked[1][:, lo:hi, :], flat[lo // 256][:].rearrange("p u c -> p c u"))
+        def gather_pair(u):
+            for h in range(2):
+                gather(flat[h][:, u, :], u, 256 + 256 * h, 512 + 256 * h)
+            for lo in (0, 768):
+                gather(words[:, lo : lo + 256, u], u, lo, lo + 256)
 
-        def quantize_s(h, lo, hi):
+        def weave(h):
+            nc.scalar.copy(words[:, 256 + 256 * h : 512 + 256 * h, :], flat[h].rearrange("p u c -> p c u"))
+
+        def quantize_s(h):
             nc.vector.quantize_mx(
-                out=s_codes[:, h * HALF + lo : h * HALF + hi].bitcast(FP8X4),
-                scales=s_bytes[:, h * HALF + lo : h * HALF + hi],
-                in_=picked[h][:, lo:hi, :].rearrange("p w u -> p (w u)").bitcast(BF16),
+                out=s_codes[:, h * HALF : (h + 1) * HALF].bitcast(FP8X4),
+                scales=s_bytes[:, h * HALF : (h + 1) * HALF],
+                in_=picked[:, h * S : (h + 1) * S].bitcast(BF16),
             )
 
         def quantize_x(i):
+            lo, hi = spans[i]
             nc.vector.quantize_mx(
-                out=x_codes[i][:].bitcast(FP8X4),
-                scales=x_bytes[i][:],
-                in_=x_grouped[i][:, :, :].rearrange("p w t -> p (w t)"),
+                out=x_codes[:, lo:hi].bitcast(FP8X4),
+                scales=x_bytes[:, lo:hi],
+                in_=x_grouped[:, 4 * lo : 4 * hi],
             )
 
         def s_pass(i):
@@ -156,12 +158,13 @@ def tile_picked_recall_bias_e_kernel(tc, xT, sT, w1_words, w1_scales, w2_words, 
             )
 
         def x_pass(i):
+            lo, hi = spans[i]
             nc.tensor.matmul_mx(
                 out=banks[i][:],
                 lhsT=w1_codes[:].bitcast(FP8X4),
                 lhsT_scale=w_bytes[:, 0:N],
-                rhs=x_codes[i][:].bitcast(FP8X4),
-                rhs_scale=x_bytes[i][:],
+                rhs=x_codes[:, lo:hi].bitcast(FP8X4),
+                rhs_scale=x_bytes[:, lo:hi],
                 start=False,
                 stop=True,
             )
@@ -180,9 +183,7 @@ def tile_picked_recall_bias_e_kernel(tc, xT, sT, w1_words, w1_scales, w2_words, 
         cast_s("v", 0, 256, 1024)
         cast_s("s", 1, 0, 352)
         cast_s("v", 1, 352, 1024)
-        gather(picked[0][:, :, 0], 0, 0, HALF)
-        gather(flat[0][:, 0, :], 0, 512, 768)
-        gather(flat[1][:, 0, :], 0, 768, 1024)
+        gather_pair(0)
         cast_s("s", 2, 0, 512)
         cast_s("s", 3, 0, 512)
         cast_s("s", 4, 0, 384)
@@ -190,36 +191,33 @@ def tile_picked_recall_bias_e_kernel(tc, xT, sT, w1_words, w1_scales, w2_words, 
         cast_s("v", 5, 0, 256)
         cast_s("s", 6, 0, 96)
         cast_s("v", 6, 96, 256)
-        gather(flat[0][:, 1, :], 1, 512, 768)
-        gather(flat[1][:, 1, :], 1, 768, 1024)
-        gather(picked[0][:, 0:256, 1], 1, 0, 256)
-        gather(picked[0][:, 256:512, 1], 1, 256, 512)
+        gather_pair(1)
         cast_x("s", 0, 0, 128)
-        weave(0, 256)
-        weave(256, 512)
+        weave(0)
+        weave(1)
         cast_x("g", 1, 0, 256)
         cast_x("s", 2, 0, 256)
         cast_x("s", 3, 0, 256)
-        quantize_s(0, 0, 256)
+        cast_x("s", 4, 0, 64)
+        quantize_s(0)
         s_pass(0)
-        quantize_x(0)
-        x_pass(0)
-        quantize_s(0, 256, 512)
         s_pass(1)
-        quantize_x(1)
-        x_pass(1)
-        quantize_s(1, 0, 512)
+        quantize_s(1)
         for i in range(2, 5):
             s_pass(i)
-        cast_x("v", 4, 0, 128)
-        for i in range(2, 5):
+        for i in range(3):
+            quantize_x(i)
+            x_pass(i)
+        cast_x("v", 4, 64, 128)
+        for i in range(3, 5):
             quantize_x(i)
             x_pass(i)
         evict("s", 0)
         evict("s", 1)
         store(0, 384)
-        for i in range(2, 4):
-            evict("s", i)
-            store(*spans[i])
-        evict("v", 4)
-        store(*spans[4])
+        evict("s", 2)
+        store(384, 640)
+        evict("v", 3)
+        store(640, 896)
+        evict("s", 4)
+        store(896, 1024)

@@ -68,18 +68,20 @@ def tile_picked_recall_bias_e_kernel(tc, xT, sT, w1_words, w1_scales, w2_words, 
 
         load_s(0)
         nc.sync.dma_start(offsets[:], offs)
-        nc.sync.dma_start(bias[:], b)
-        for i in range(1, len(s_chunks)):
+        load_scales(1)
+        load_s(1)
+        load_s(2)
+        load_scales(0)
+        for i in range(3, 7):
             load_s(i)
         load_x(0)
         load_x(1)
-        load_codes(1)
-        load_scales(1)
         load_x(2)
+        load_codes(1)
+        nc.sync.dma_start(bias[:], b)
         load_x(3)
-        load_x(4)
         load_codes(0)
-        load_scales(0)
+        load_x(4)
 
         pairs = [keep.tile([P, 2 * T], BF16, name=f"pairs{u}", align_bytes=64) for u in range(2)]
         words = picked[:].bitcast(U32).rearrange("p (w u) -> p w u", u=2)
@@ -197,8 +199,8 @@ def tile_picked_recall_bias_e_kernel(tc, xT, sT, w1_words, w1_scales, w2_words, 
         weave(1)
         cast_x("g", 1, 0, 256)
         cast_x("s", 2, 0, 256)
-        cast_x("s", 3, 0, 256)
-        cast_x("s", 4, 0, 64)
+        cast_x("s", 3, 0, 128)
+        cast_x("s", 3, 128, 256)
         quantize_s(0)
         s_pass(0)
         s_pass(1)
@@ -208,13 +210,14 @@ def tile_picked_recall_bias_e_kernel(tc, xT, sT, w1_words, w1_scales, w2_words, 
         for i in range(3):
             quantize_x(i)
             x_pass(i)
-        cast_x("v", 4, 64, 128)
+        cast_x("v", 4, 0, 128)
         for i in range(3, 5):
             quantize_x(i)
             x_pass(i)
         evict("s", 0)
+        store(0, 128)
         evict("s", 1)
-        store(0, 384)
+        store(128, 384)
         evict("s", 2)
         store(384, 640)
         evict("v", 3)

@@ -14,11 +14,27 @@ U8 = mybir.dt.uint8
 FP8X4 = mybir.dt.float8_e4m3fn_x4
 COPY = mybir.ActivationFunctionType.Copy
 IDENTITY = mybir.ActivationFunctionType.Identity
-
-P = 128
-HALF = S // 2
 MULT = mybir.AluOpType.mult
 ADD = mybir.AluOpType.add
+
+P = 128
+QUAD = 32
+PACK = 4
+PER_COLUMN = 16
+QUARTER = S // 4
+
+S_CHUNKS = [
+    (0, 0, 1024, 256),
+    (0, 1024, 2048, 352),
+    (1, 0, 512, 512),
+    (1, 512, 1024, 512),
+    (1, 1024, 1536, 384),
+    (1, 1536, 1792, 0),
+    (1, 1792, 2048, 96),
+]
+X_CHUNKS = [(0, 128), (128, 384), (384, 640), (640, 896), (896, 1024)]
+LAST_SCALAR_SHARE = 64
+BANKS = [(0, 256), (256, 512), (512, 768), (768, 896), (896, 1024)]
 
 
 def tile_picked_recall_bias_e_kernel(tc, xT, sT, w1_words, w1_scales, w2_words, w2_scales, b, offs, out):
@@ -27,200 +43,177 @@ def tile_picked_recall_bias_e_kernel(tc, xT, sT, w1_words, w1_scales, w2_words, 
         keep = ctx.enter_context(tc.tile_pool(name="keep", bufs=1))
         psum = ctx.enter_context(tc.psum_pool(name="psum", bufs=1))
 
-        offsets = keep.tile([P, S // 16], U16, name="offsets")
+        offsets = keep.tile([P, S // PER_COLUMN], U16, name="offsets")
         w1_codes = keep.tile([P, N], U32, name="w1_codes", align_bytes=64)
         w2_codes = keep.tile([P, N], U32, name="w2_codes", align_bytes=64)
         w_bytes = keep.tile([P, 2 * N], U8, name="w_bytes", align_bytes=64)
-        bias = keep.tile([P, 1], F32, name="bias")
+        w1_bytes = w_bytes[:, 0:N]
+        w2_bytes = w_bytes[:, N : 2 * N]
+        bias_rows = keep.tile([P, QUAD], F32, name="bias_rows", align_bytes=64)
+        bias_cols = keep.tile([P, QUAD], F32, name="bias_cols", align_bytes=64)
+        bias = bias_cols[:, 0:1]
 
-        s_rows = sT.rearrange("(p t) w -> p t w", t=4)
-        x_rows = xT.rearrange("(p t) w -> p t w", t=4)
-        s_chunks = [(0, 0, 1024), (0, 1024, 2048), (1, 0, 512), (1, 512, 1024), (1, 1024, 1536), (1, 1536, 1792), (1, 1792, 2048)]
-        x_chunks = [(0, 128), (128, 384), (384, 640), (640, 896), (896, 1024)]
-        spans = x_chunks
-        s_raw = [keep.tile([P, 2, hi - lo], F32, name=f"s_raw{i}") for i, (u, lo, hi) in enumerate(s_chunks)]
+        s_rows = sT.rearrange("(p t) w -> p t w", t=PACK)
+        x_rows = xT.rearrange("(p t) w -> p t w", t=PACK)
+        s_raw = [keep.tile([P, 2, hi - lo], F32, name=f"s_raw{i}") for i, (u, lo, hi, share) in enumerate(S_CHUNKS)]
+
         picked = keep.tile([P, 2 * S], F32, name="picked", align_bytes=64)
-        x_raw = [picked[:, 768:1280].rearrange("p (t w) -> p t w", t=4)]
-        x_raw.extend(keep.tile([P, 4, hi - lo], F32, name=f"x_raw{lo}")[:] for lo, hi in x_chunks[1:])
-        whole = x_raw[3].rearrange("p t w -> p (t w)")
+        x_raw = [picked[:, S - QUARTER : S + QUARTER].rearrange("p (t w) -> p t w", t=PACK)]
+        x_raw.extend(keep.tile([P, PACK, hi - lo], F32, name=f"x_raw{lo}")[:] for lo, hi in X_CHUNKS[1:])
+        result = x_raw[3].rearrange("p t w -> p (t w)")
 
         def load_s(i):
-            u, lo, hi = s_chunks[i]
+            u, lo, hi, share = S_CHUNKS[i]
             nc.sync.dma_start(s_raw[i][:], s_rows[:, 2 * u : 2 * u + 2, lo:hi])
 
-        def load_codes(side):
-            codes, words = ((w1_codes, w1_words), (w2_codes, w2_words))[side]
+        def load_x(j):
+            lo, hi = X_CHUNKS[j]
+            nc.sync.dma_start(x_raw[j], x_rows[:, :, lo:hi])
+
+        def load_codes(codes, words):
             nc.sync.dma_start(codes[:].bitcast(I32), words[0].rearrange("p n t -> p (n t)").bitcast(I32))
 
+        def load_scales(plane, scales):
+            for q in range(P // QUAD):
+                nc.sync.dma_start(plane[QUAD * q : QUAD * q + 4, :].bitcast(I32), scales[0, 4 * q : 4 * q + 4, :].bitcast(I32))
+
+        nc.vector.memset(bias_rows[:], 0.0)
         nc.vector.memset(w_bytes[:].bitcast(I32), 0)
-
-        def load_scales(side):
-            scales = (w1_scales, w2_scales)[side]
-            for quad in range(4):
-                nc.sync.dma_start(
-                    w_bytes[32 * quad : 32 * quad + 4, side * N : (side + 1) * N].bitcast(I32),
-                    scales[0, 4 * quad : 4 * quad + 4, :].bitcast(I32),
-                )
-
-        def load_x(j):
-            lo, hi = x_chunks[j]
-            nc.sync.dma_start(x_raw[j], x_rows[:, :, lo:hi])
 
         load_s(0)
         nc.sync.dma_start(offsets[:], offs)
-        load_scales(1)
+        nc.sync.dma_start(bias_rows[0:P:QUAD, :], b.rearrange("(q j) one -> q (j one)", j=QUAD))
+        load_scales(w2_bytes, w2_scales)
         load_s(1)
         load_s(2)
-        load_scales(0)
-        for i in range(3, 7):
+        load_scales(w1_bytes, w1_scales)
+        for i in range(3, len(S_CHUNKS)):
             load_s(i)
-        load_x(0)
-        load_x(1)
-        load_x(2)
-        load_codes(1)
-        nc.sync.dma_start(bias[:], b)
+        for j in range(3):
+            load_x(j)
+        load_codes(w2_codes, w2_words)
         load_x(3)
-        load_codes(0)
+        load_codes(w1_codes, w1_words)
         load_x(4)
 
         pairs = [keep.tile([P, 2 * T], BF16, name=f"pairs{u}", align_bytes=64) for u in range(2)]
-        words = picked[:].bitcast(U32).rearrange("p (w u) -> p w u", u=2)
+        picked_words = picked[:].bitcast(U32).rearrange("p (w u) -> p w u", u=2)
         s_codes = keep.tile([P, S], U32, name="s_codes", align_bytes=64)
         s_bytes = keep.tile([P, S], U8, name="s_bytes", align_bytes=64)
-        x_grouped = keep.tile([P, 4 * S], BF16, name="x_grouped", align_bytes=64)
-        flat_late = keep.tile([P, 2, 256], U32, name="flat_late", align_bytes=64)
-        flat = [x_grouped[:, 4 * 384 : 4 * 640].bitcast(U32).rearrange("p (u c) -> p u c", u=2), flat_late[:]]
+        x_grouped = keep.tile([P, PACK * S], BF16, name="x_grouped", align_bytes=64)
+        second_runs = keep.tile([P, 2, QUARTER], U32, name="second_runs", align_bytes=64)
+        third_lo, third_hi = X_CHUNKS[2]
+        first_runs = x_grouped[:, PACK * third_lo : PACK * third_hi].bitcast(U32).rearrange("p (u c) -> p u c", u=2)
+        runs = {1: first_runs, 2: second_runs[:]}
         x_codes = keep.tile([P, S], U32, name="x_codes", align_bytes=64)
         x_bytes = keep.tile([P, S], U8, name="x_bytes", align_bytes=64)
-        banks = [psum.tile([P, hi - lo], F32, name=f"bank{i}") for i, (lo, hi) in enumerate(spans)]
+        banks = [psum.tile([P, hi - lo], F32, name=f"bank{i}") for i, (lo, hi) in enumerate(BANKS)]
 
-        def result(lo, hi):
-            return whole[:, lo:hi]
+        def scalar_cast(dst, src):
+            nc.scalar.activation(dst, src, COPY)
 
-        def cast_s(engine, i, a, z):
-            u, lo, hi = s_chunks[i]
-            dst = pairs[u][:].rearrange("p (w e) -> p w e", e=2)[:, lo + a : lo + z, :]
-            src = s_raw[i][:, :, a:z].rearrange("p e w -> p w e")
-            if engine == "v":
-                nc.vector.tensor_copy(dst, src)
-            else:
-                nc.scalar.activation(dst, src, COPY)
+        def cast_s(i):
+            u, lo, hi, share = S_CHUNKS[i]
+            dst = pairs[u][:].rearrange("p (w e) -> p w e", e=2)[:, lo:hi, :]
+            src = s_raw[i][:].rearrange("p e w -> p w e")
+            if share > 0:
+                scalar_cast(dst[:, 0:share, :], src[:, 0:share, :])
+            if share < hi - lo:
+                nc.vector.tensor_copy(dst[:, share:, :], src[:, share:, :])
 
-        def cast_x(engine, j, a, z):
-            lo = x_chunks[j][0]
-            dst = x_grouped[:, 4 * (lo + a) : 4 * (lo + z)].rearrange("p (c t) -> p c t", t=4)
-            src = x_raw[j][:, :, a:z]
-            if engine == "g":
-                nc.gpsimd.tensor_scalar(dst, src.rearrange("p t c -> p c t"), 1.0, 0.0, MULT, ADD)
-                return
-            dst = dst.rearrange("p (c i) t -> p c t i", i=4)
-            src = src.rearrange("p t (c i) -> p c t i", i=4)
-            if engine == "v":
-                nc.vector.tensor_copy(dst, src)
-            else:
-                nc.scalar.activation(dst, src, COPY)
+        def x_target(j, a, z):
+            lo = X_CHUNKS[j][0]
+            return x_grouped[:, PACK * (lo + a) : PACK * (lo + z)].rearrange("p (c t) -> p c t", t=PACK)
 
-        def gather(dst, u, lo, hi):
-            nc.vector.tensor_copy(dst, pairs[u][:].bitcast(U32).indirect(offsets[:, lo // 16 : hi // 16]))
-
-        def gather_pair(u):
-            for h in range(2):
-                gather(flat[h][:, u, :], u, 256 + 256 * h, 512 + 256 * h)
-            for lo in (0, 768):
-                gather(words[:, lo : lo + 256, u], u, lo, lo + 256)
-
-        def weave(h):
-            nc.scalar.copy(words[:, 256 + 256 * h : 512 + 256 * h, :], flat[h].rearrange("p u c -> p c u"))
-
-        def quantize_s(h):
-            nc.vector.quantize_mx(
-                out=s_codes[:, h * HALF : (h + 1) * HALF].bitcast(FP8X4),
-                scales=s_bytes[:, h * HALF : (h + 1) * HALF],
-                in_=picked[:, h * S : (h + 1) * S].bitcast(BF16),
+        def cast_x(cast, j, a, z):
+            cast(
+                x_target(j, a, z).rearrange("p (c i) t -> p c t i", i=4),
+                x_raw[j][:, :, a:z].rearrange("p t (c i) -> p c t i", i=4),
             )
 
-        def quantize_x(i):
-            lo, hi = spans[i]
+        def gather_pair(u):
+            window = pairs[u][:].bitcast(U32)
+            for quarter in (1, 2, 0, 3):
+                lo, hi = quarter * QUARTER, (quarter + 1) * QUARTER
+                dst = runs[quarter][:, u, :] if quarter in runs else picked_words[:, lo:hi, u]
+                nc.vector.tensor_copy(dst, window.indirect(offsets[:, lo // PER_COLUMN : hi // PER_COLUMN]))
+
+        def weave(quarter):
+            nc.scalar.copy(picked_words[:, quarter * QUARTER : (quarter + 1) * QUARTER, :], runs[quarter].rearrange("p u c -> p c u"))
+
+        def quantize_s(lo, hi):
             nc.vector.quantize_mx(
-                out=x_codes[:, lo:hi].bitcast(FP8X4),
-                scales=x_bytes[:, lo:hi],
-                in_=x_grouped[:, 4 * lo : 4 * hi],
+                out=s_codes[:, lo:hi].bitcast(FP8X4),
+                scales=s_bytes[:, lo:hi],
+                in_=picked[:, 2 * lo : 2 * hi].bitcast(BF16),
             )
 
         def s_pass(i):
-            lo, hi = spans[i]
+            lo, hi = BANKS[i]
             nc.tensor.matmul_mx(
                 out=banks[i][:],
                 lhsT=w2_codes[:].bitcast(FP8X4),
-                lhsT_scale=w_bytes[:, N : 2 * N],
+                lhsT_scale=w2_bytes,
                 rhs=s_codes[:, lo:hi].bitcast(FP8X4),
                 rhs_scale=s_bytes[:, lo:hi],
                 start=True,
                 stop=False,
             )
 
-        def x_pass(i):
-            lo, hi = spans[i]
+        def x_quantize_and_pass(i):
+            lo, hi = BANKS[i]
+            nc.vector.quantize_mx(
+                out=x_codes[:, lo:hi].bitcast(FP8X4),
+                scales=x_bytes[:, lo:hi],
+                in_=x_grouped[:, PACK * lo : PACK * hi],
+            )
             nc.tensor.matmul_mx(
                 out=banks[i][:],
                 lhsT=w1_codes[:].bitcast(FP8X4),
-                lhsT_scale=w_bytes[:, 0:N],
+                lhsT_scale=w1_bytes,
                 rhs=x_codes[:, lo:hi].bitcast(FP8X4),
                 rhs_scale=x_bytes[:, lo:hi],
                 start=False,
                 stop=True,
             )
 
-        def evict(engine, i):
-            lo, hi = spans[i]
-            if engine == "v":
-                nc.vector.tensor_scalar_add(result(lo, hi), banks[i][:], bias[:])
-            else:
-                nc.scalar.activation(result(lo, hi), banks[i][:], IDENTITY, bias=bias[:])
-
         def store(lo, hi):
-            nc.sync.dma_start(out[:, lo:hi], result(lo, hi))
+            nc.sync.dma_start(out[:, lo:hi], result[:, lo:hi])
 
-        cast_s("s", 0, 0, 256)
-        cast_s("v", 0, 256, 1024)
-        cast_s("s", 1, 0, 352)
-        cast_s("v", 1, 352, 1024)
+        cast_s(0)
+        cast_s(1)
+        nc.vector.transpose(bias_cols[:], bias_rows[:])
         gather_pair(0)
-        cast_s("s", 2, 0, 512)
-        cast_s("s", 3, 0, 512)
-        cast_s("s", 4, 0, 384)
-        cast_s("v", 4, 384, 512)
-        cast_s("v", 5, 0, 256)
-        cast_s("s", 6, 0, 96)
-        cast_s("v", 6, 96, 256)
+        for i in range(2, len(S_CHUNKS)):
+            cast_s(i)
         gather_pair(1)
-        cast_x("s", 0, 0, 128)
-        weave(0)
+
+        widths = [hi - lo for lo, hi in X_CHUNKS]
+        cast_x(scalar_cast, 0, 0, widths[0])
         weave(1)
-        cast_x("g", 1, 0, 256)
-        cast_x("s", 2, 0, 256)
-        cast_x("s", 3, 0, 128)
-        cast_x("s", 3, 128, 256)
-        quantize_s(0)
-        s_pass(0)
-        s_pass(1)
-        quantize_s(1)
-        for i in range(2, 5):
+        weave(2)
+        nc.gpsimd.tensor_scalar(x_target(1, 0, widths[1]), x_raw[1].rearrange("p t c -> p c t"), 1.0, 0.0, MULT, ADD)
+        cast_x(scalar_cast, 2, 0, widths[2])
+        cast_x(scalar_cast, 3, 0, widths[3])
+        cast_x(scalar_cast, 4, 0, LAST_SCALAR_SHARE)
+
+        for i in range(2):
+            quantize_s(*BANKS[i])
             s_pass(i)
+        x_quantize_and_pass(0)
+        quantize_s(S // 2, S)
+        for i in range(2, len(BANKS)):
+            s_pass(i)
+        x_quantize_and_pass(1)
+        cast_x(nc.vector.tensor_copy, 4, LAST_SCALAR_SHARE, widths[4])
+        for i in range(2, len(BANKS)):
+            x_quantize_and_pass(i)
+
         for i in range(3):
-            quantize_x(i)
-            x_pass(i)
-        cast_x("v", 4, 0, 128)
-        for i in range(3, 5):
-            quantize_x(i)
-            x_pass(i)
-        evict("s", 0)
-        store(0, 128)
-        evict("s", 1)
-        store(128, 384)
-        evict("s", 2)
-        store(384, 640)
-        evict("v", 3)
-        store(640, 896)
-        evict("s", 4)
-        store(896, 1024)
+            lo, hi = BANKS[i]
+            nc.scalar.activation(result[:, lo:hi], banks[i][:], IDENTITY, bias=bias)
+            store(lo, hi)
+        for i in range(3, len(BANKS)):
+            lo, hi = BANKS[i]
+            nc.vector.tensor_scalar_add(result[:, lo:hi], banks[i][:], bias)
+        store(BANKS[3][0], S)

@@ -23,18 +23,7 @@ PACK = 4
 PER_COLUMN = 16
 QUARTER = S // 4
 
-S_CHUNKS = [
-    (0, 0, 1024, 256),
-    (0, 1024, 2048, 352),
-    (1, 0, 512, 512),
-    (1, 512, 1024, 512),
-    (1, 1024, 1536, 384),
-    (1, 1536, 1792, 0),
-    (1, 1792, 2048, 96),
-]
 X_CHUNKS = [(0, 128), (128, 384), (384, 640), (640, 896), (896, 1024)]
-LAST_SCALAR_SHARE = 64
-BANKS = [(0, 256), (256, 512), (512, 768), (768, 896), (896, 1024)]
 
 
 def tile_picked_recall_bias_e_kernel(tc, xT, sT, w1_words, w1_scales, w2_words, w2_scales, b, offs, out):
@@ -55,20 +44,17 @@ def tile_picked_recall_bias_e_kernel(tc, xT, sT, w1_words, w1_scales, w2_words, 
 
         s_rows = sT.rearrange("(p t) w -> p t w", t=PACK)
         x_rows = xT.rearrange("(p t) w -> p t w", t=PACK)
-        s_raw = [keep.tile([P, 2, hi - lo], F32, name=f"s_raw{i}") for i, (u, lo, hi, share) in enumerate(S_CHUNKS)]
+        planes = [keep.tile([P, T], F32, name=f"plane{t}") for t in range(PACK)]
+        x_raw = [keep.tile([P, PACK * (hi - lo)], F32, name=f"x_raw{lo}") for lo, hi in X_CHUNKS]
+        staged = x_raw[3]
+        results = [staged[:, lo:hi] for lo, hi in X_CHUNKS]
 
-        picked = keep.tile([P, 2 * S], F32, name="picked", align_bytes=64)
-        x_raw = [picked[:, S - QUARTER : S + QUARTER].rearrange("p (t w) -> p t w", t=PACK)]
-        x_raw.extend(keep.tile([P, PACK, hi - lo], F32, name=f"x_raw{lo}")[:] for lo, hi in X_CHUNKS[1:])
-        result = x_raw[3].rearrange("p t w -> p (t w)")
-
-        def load_s(i):
-            u, lo, hi, share = S_CHUNKS[i]
-            nc.sync.dma_start(s_raw[i][:], s_rows[:, 2 * u : 2 * u + 2, lo:hi])
+        def load_s(t):
+            nc.sync.dma_start(planes[t][:], s_rows[:, t, :])
 
         def load_x(j):
             lo, hi = X_CHUNKS[j]
-            nc.sync.dma_start(x_raw[j], x_rows[:, :, lo:hi])
+            nc.sync.dma_start(x_raw[j][:].rearrange("p (t w) -> p t w", t=PACK), x_rows[:, :, lo:hi])
 
         def load_codes(codes, words):
             nc.sync.dma_start(codes[:].bitcast(I32), words[0].rearrange("p n t -> p (n t)").bitcast(I32))
@@ -82,74 +68,65 @@ def tile_picked_recall_bias_e_kernel(tc, xT, sT, w1_words, w1_scales, w2_words, 
 
         load_s(0)
         nc.sync.dma_start(offsets[:], offs)
+        load_s(1)
         nc.sync.dma_start(bias_rows[0:P:QUAD, :], b.rearrange("(q j) one -> q (j one)", j=QUAD))
         load_scales(w2_bytes, w2_scales)
-        load_s(1)
         load_s(2)
         load_scales(w1_bytes, w1_scales)
-        for i in range(3, len(S_CHUNKS)):
-            load_s(i)
-        for j in range(3):
-            load_x(j)
+        load_s(3)
+        load_x(0)
         load_codes(w2_codes, w2_words)
-        load_x(3)
+        load_x(1)
+        load_x(2)
         load_codes(w1_codes, w1_words)
+        load_x(3)
         load_x(4)
 
-        pairs = [keep.tile([P, 2 * T], BF16, name=f"pairs{u}", align_bytes=64) for u in range(2)]
-        picked_words = picked[:].bitcast(U32).rearrange("p (w u) -> p w u", u=2)
+        halves = [keep.tile([P, 2 * PACK * QUARTER], BF16, name=f"picked{h}", align_bytes=64) for h in range(2)]
+        picked = [halves[q // 2][:, (q % 2) * PACK * QUARTER : (q % 2 + 1) * PACK * QUARTER] for q in range(4)]
+        flat = [keep.tile([P, 4 * QUARTER], BF16, name=f"flat{u}", align_bytes=64) for u in range(2)]
         s_codes = keep.tile([P, S], U32, name="s_codes", align_bytes=64)
         s_bytes = keep.tile([P, S], U8, name="s_bytes", align_bytes=64)
-        x_grouped = keep.tile([P, PACK * S], BF16, name="x_grouped", align_bytes=64)
-        second_runs = keep.tile([P, 2, QUARTER], U32, name="second_runs", align_bytes=64)
-        third_lo, third_hi = X_CHUNKS[2]
-        first_runs = x_grouped[:, PACK * third_lo : PACK * third_hi].bitcast(U32).rearrange("p (u c) -> p u c", u=2)
-        runs = {1: first_runs, 2: second_runs[:]}
+        x_grouped = [keep.tile([P, PACK * (hi - lo)], BF16, name=f"x_grouped{lo}", align_bytes=64) for lo, hi in X_CHUNKS]
         x_codes = keep.tile([P, S], U32, name="x_codes", align_bytes=64)
         x_bytes = keep.tile([P, S], U8, name="x_bytes", align_bytes=64)
-        banks = [psum.tile([P, hi - lo], F32, name=f"bank{i}") for i, (lo, hi) in enumerate(BANKS)]
+        banks = [psum.tile([P, hi - lo], F32, name=f"bank{i}") for i, (lo, hi) in enumerate(X_CHUNKS)]
 
         def scalar_cast(dst, src):
             nc.scalar.activation(dst, src, COPY)
 
-        def cast_s(i):
-            u, lo, hi, share = S_CHUNKS[i]
-            dst = pairs[u][:].rearrange("p (w e) -> p w e", e=2)[:, lo:hi, :]
-            src = s_raw[i][:].rearrange("p e w -> p w e")
-            if share > 0:
-                scalar_cast(dst[:, 0:share, :], src[:, 0:share, :])
-            if share < hi - lo:
-                nc.vector.tensor_copy(dst[:, share:, :], src[:, share:, :])
+        def looked_up(t, lo, hi):
+            return planes[t][:].indirect(offsets[:, lo * QUARTER // PER_COLUMN : hi * QUARTER // PER_COLUMN])
 
-        def x_target(j, a, z):
-            lo = X_CHUNKS[j][0]
-            return x_grouped[:, PACK * (lo + a) : PACK * (lo + z)].rearrange("p (c t) -> p c t", t=PACK)
+        def slot(q, lo, hi):
+            return picked[q].rearrange("p (c t) -> p c t", t=PACK)[:, :, lo:hi]
+
+        def gather_early(t):
+            nc.vector.tensor_copy(halves[0][:].rearrange("p (c t) -> p c t", t=PACK)[:, :, t], looked_up(t, 0, 2))
+            e = t % 2
+            scalar_cast(flat[t // 2][:, 2 * e * QUARTER : 2 * (e + 1) * QUARTER], looked_up(t, 2, 4))
+
+        def gather_last():
+            nc.vector.tensor_copy(halves[0][:].rearrange("p (c t) -> p c t", t=PACK)[:, :, 3], looked_up(3, 0, 2))
+            for q in (2, 3):
+                scalar_cast(flat[1][:, q * QUARTER : (q + 1) * QUARTER], looked_up(3, q, q + 1))
+
+        def weave(q, u):
+            src = flat[u][:].rearrange("p (e c) -> p c e", e=2)[:, (q - 2) * QUARTER : (q - 1) * QUARTER, :]
+            nc.vector.tensor_copy(slot(q, 2 * u, 2 * u + 2), src)
 
         def cast_x(cast, j, a, z):
             cast(
-                x_target(j, a, z).rearrange("p (c i) t -> p c t i", i=4),
-                x_raw[j][:, :, a:z].rearrange("p t (c i) -> p c t i", i=4),
+                x_grouped[j][:, PACK * a : PACK * z].rearrange("p (c i t) -> p c t i", i=4, t=PACK),
+                x_raw[j][:].rearrange("p (t c) -> p t c", t=PACK)[:, :, a:z].rearrange("p t (c i) -> p c t i", i=4),
             )
 
-        def gather_pair(u):
-            window = pairs[u][:].bitcast(U32)
-            for quarter in (1, 2, 0, 3):
-                lo, hi = quarter * QUARTER, (quarter + 1) * QUARTER
-                dst = runs[quarter][:, u, :] if quarter in runs else picked_words[:, lo:hi, u]
-                nc.vector.tensor_copy(dst, window.indirect(offsets[:, lo // PER_COLUMN : hi // PER_COLUMN]))
-
-        def weave(quarter):
-            nc.scalar.copy(picked_words[:, quarter * QUARTER : (quarter + 1) * QUARTER, :], runs[quarter].rearrange("p u c -> p c u"))
-
-        def quantize_s(lo, hi):
-            nc.vector.quantize_mx(
-                out=s_codes[:, lo:hi].bitcast(FP8X4),
-                scales=s_bytes[:, lo:hi],
-                in_=picked[:, 2 * lo : 2 * hi].bitcast(BF16),
-            )
+        def quantize_s(q):
+            lo, hi = 2 * q * QUARTER, 2 * (q + 1) * QUARTER
+            nc.vector.quantize_mx(out=s_codes[:, lo:hi].bitcast(FP8X4), scales=s_bytes[:, lo:hi], in_=halves[q][:])
 
         def s_pass(i):
-            lo, hi = BANKS[i]
+            lo, hi = X_CHUNKS[i]
             nc.tensor.matmul_mx(
                 out=banks[i][:],
                 lhsT=w2_codes[:].bitcast(FP8X4),
@@ -160,13 +137,16 @@ def tile_picked_recall_bias_e_kernel(tc, xT, sT, w1_words, w1_scales, w2_words, 
                 stop=False,
             )
 
+        def x_quantize(i):
+            lo, hi = X_CHUNKS[i]
+            nc.vector.quantize_mx(out=x_codes[:, lo:hi].bitcast(FP8X4), scales=x_bytes[:, lo:hi], in_=x_grouped[i][:])
+
         def x_quantize_and_pass(i):
-            lo, hi = BANKS[i]
-            nc.vector.quantize_mx(
-                out=x_codes[:, lo:hi].bitcast(FP8X4),
-                scales=x_bytes[:, lo:hi],
-                in_=x_grouped[:, PACK * lo : PACK * hi],
-            )
+            x_quantize(i)
+            x_pass(i)
+
+        def x_pass(i):
+            lo, hi = X_CHUNKS[i]
             nc.tensor.matmul_mx(
                 out=banks[i][:],
                 lhsT=w1_codes[:].bitcast(FP8X4),
@@ -177,43 +157,41 @@ def tile_picked_recall_bias_e_kernel(tc, xT, sT, w1_words, w1_scales, w2_words, 
                 stop=True,
             )
 
-        def store(lo, hi):
-            nc.sync.dma_start(out[:, lo:hi], result[:, lo:hi])
+        def scalar_read(i):
+            nc.scalar.activation(results[i], banks[i][:], IDENTITY, bias=bias)
+            lo, hi = X_CHUNKS[i]
+            nc.sync.dma_start(out[:, lo:hi], results[i])
 
-        cast_s(0)
-        cast_s(1)
+        gather_early(0)
         nc.vector.transpose(bias_cols[:], bias_rows[:])
-        gather_pair(0)
-        for i in range(2, len(S_CHUNKS)):
-            cast_s(i)
-        gather_pair(1)
-
-        widths = [hi - lo for lo, hi in X_CHUNKS]
-        cast_x(scalar_cast, 0, 0, widths[0])
-        weave(1)
-        weave(2)
-        nc.gpsimd.tensor_scalar(x_target(1, 0, widths[1]), x_raw[1].rearrange("p t c -> p c t"), 1.0, 0.0, MULT, ADD)
-        cast_x(scalar_cast, 2, 0, widths[2])
-        cast_x(scalar_cast, 3, 0, widths[3])
-        cast_x(scalar_cast, 4, 0, LAST_SCALAR_SHARE)
-
-        for i in range(2):
-            quantize_s(*BANKS[i])
+        gather_early(1)
+        for q in (2, 3):
+            weave(q, 0)
+        gather_early(2)
+        gather_last()
+        nc.gpsimd.tensor_scalar(
+            x_grouped[0][:].rearrange("p (c t) -> p c t", t=PACK), x_raw[0][:].rearrange("p (t c) -> p c t", t=PACK), 1.0, 0.0, MULT, ADD
+        )
+        weave(2, 1)
+        quantize_s(0)
+        s_pass(0)
+        s_pass(1)
+        weave(3, 1)
+        cast_x(scalar_cast, 1, 0, 256)
+        cast_x(scalar_cast, 2, 0, 256)
+        cast_x(scalar_cast, 3, 0, 128)
+        x_quantize(0)
+        quantize_s(1)
+        for i in (2, 3, 4):
             s_pass(i)
-        x_quantize_and_pass(0)
-        quantize_s(S // 2, S)
-        for i in range(2, len(BANKS)):
-            s_pass(i)
+        x_pass(0)
         x_quantize_and_pass(1)
-        cast_x(nc.vector.tensor_copy, 4, LAST_SCALAR_SHARE, widths[4])
-        for i in range(2, len(BANKS)):
-            x_quantize_and_pass(i)
-
-        for i in range(3):
-            lo, hi = BANKS[i]
-            nc.scalar.activation(result[:, lo:hi], banks[i][:], IDENTITY, bias=bias)
-            store(lo, hi)
-        for i in range(3, len(BANKS)):
-            lo, hi = BANKS[i]
-            nc.vector.tensor_scalar_add(result[:, lo:hi], banks[i][:], bias)
-        store(BANKS[3][0], S)
+        x_quantize_and_pass(2)
+        cast_x(nc.vector.tensor_copy, 3, 128, 256)
+        cast_x(nc.vector.tensor_copy, 4, 0, 128)
+        x_quantize_and_pass(3)
+        x_quantize_and_pass(4)
+        for i in range(4):
+            scalar_read(i)
+        nc.vector.tensor_scalar_add(results[4], banks[4][:], bias)
+        nc.sync.dma_start(out[:, 896:1024], results[4])

@@ -14,8 +14,6 @@ U8 = mybir.dt.uint8
 FP8X4 = mybir.dt.float8_e4m3fn_x4
 COPY = mybir.ActivationFunctionType.Copy
 IDENTITY = mybir.ActivationFunctionType.Identity
-MULT = mybir.AluOpType.mult
-ADD = mybir.AluOpType.add
 
 P = 128
 QUAD = 32
@@ -23,7 +21,8 @@ PACK = 4
 PER_COLUMN = 16
 QUARTER = S // 4
 
-X_CHUNKS = [(0, 128), (128, 384), (384, 640), (640, 896), (896, 1024)]
+X_CHUNKS = [(0, 512), (512, 768), (768, 896), (896, 1024)]
+BANKS = [(0, 256), (256, 512), (512, 768), (768, 896), (896, 1024)]
 
 
 def tile_picked_recall_bias_e_kernel(tc, xT, sT, w1_words, w1_scales, w2_words, w2_scales, b, offs, out):
@@ -45,16 +44,18 @@ def tile_picked_recall_bias_e_kernel(tc, xT, sT, w1_words, w1_scales, w2_words, 
         s_rows = sT.rearrange("(p t) w -> p t w", t=PACK)
         x_rows = xT.rearrange("(p t) w -> p t w", t=PACK)
         planes = [keep.tile([P, T], F32, name=f"plane{t}") for t in range(PACK)]
-        x_raw = [keep.tile([P, PACK * (hi - lo)], F32, name=f"x_raw{lo}") for lo, hi in X_CHUNKS]
-        staged = x_raw[3]
-        results = [staged[:, lo:hi] for lo, hi in X_CHUNKS]
+        result = keep.tile([P, S], F32, name="result")
+        x_raw = [keep.tile([P, PACK * (hi - lo)], F32, name=f"x_raw{lo}")[:].rearrange("p (t w) -> p t w", t=PACK) for lo, hi in X_CHUNKS[:2]]
+        x_raw.append(result[:].rearrange("p (t w) -> p t w", t=PACK)[:, :, 0:128])
+        x_raw.append(keep.tile([P, PACK * 128], F32, name="x_raw_last")[:].rearrange("p (t w) -> p t w", t=PACK))
+        results = [result[:, lo:hi] for lo, hi in BANKS]
 
         def load_s(t):
             nc.sync.dma_start(planes[t][:], s_rows[:, t, :])
 
         def load_x(j):
             lo, hi = X_CHUNKS[j]
-            nc.sync.dma_start(x_raw[j][:].rearrange("p (t w) -> p t w", t=PACK), x_rows[:, :, lo:hi])
+            nc.sync.dma_start(x_raw[j], x_rows[:, :, lo:hi])
 
         def load_codes(codes, words):
             nc.sync.dma_start(codes[:].bitcast(I32), words[0].rearrange("p n t -> p (n t)").bitcast(I32))
@@ -77,20 +78,23 @@ def tile_picked_recall_bias_e_kernel(tc, xT, sT, w1_words, w1_scales, w2_words, 
         load_x(0)
         load_codes(w2_codes, w2_words)
         load_x(1)
-        load_x(2)
         load_codes(w1_codes, w1_words)
+        load_x(2)
         load_x(3)
-        load_x(4)
 
         halves = [keep.tile([P, 2 * PACK * QUARTER], BF16, name=f"picked{h}", align_bytes=64) for h in range(2)]
         picked = [halves[q // 2][:, (q % 2) * PACK * QUARTER : (q % 2 + 1) * PACK * QUARTER] for q in range(4)]
-        flat = [keep.tile([P, 4 * QUARTER], BF16, name=f"flat{u}", align_bytes=64) for u in range(2)]
+        flat_first = keep.tile([P, 4 * QUARTER], BF16, name="flat_first", align_bytes=64)
+        flat_second = {
+            2: keep.tile([P, 2 * QUARTER], BF16, name="flat_second2", align_bytes=64),
+            3: keep.tile([P, 2 * QUARTER], BF16, name="flat_second3", align_bytes=64),
+        }
         s_codes = keep.tile([P, S], U32, name="s_codes", align_bytes=64)
         s_bytes = keep.tile([P, S], U8, name="s_bytes", align_bytes=64)
-        x_grouped = [keep.tile([P, PACK * (hi - lo)], BF16, name=f"x_grouped{lo}", align_bytes=64) for lo, hi in X_CHUNKS]
+        x_grouped = [keep.tile([P, PACK * (hi - lo)], BF16, name=f"x_grouped{lo}", align_bytes=64) for lo, hi in BANKS]
         x_codes = keep.tile([P, S], U32, name="x_codes", align_bytes=64)
         x_bytes = keep.tile([P, S], U8, name="x_bytes", align_bytes=64)
-        banks = [psum.tile([P, hi - lo], F32, name=f"bank{i}") for i, (lo, hi) in enumerate(X_CHUNKS)]
+        banks = [psum.tile([P, hi - lo], F32, name=f"bank{i}") for i, (lo, hi) in enumerate(BANKS)]
 
         def scalar_cast(dst, src):
             nc.scalar.activation(dst, src, COPY)
@@ -101,32 +105,33 @@ def tile_picked_recall_bias_e_kernel(tc, xT, sT, w1_words, w1_scales, w2_words, 
         def slot(q, lo, hi):
             return picked[q].rearrange("p (c t) -> p c t", t=PACK)[:, :, lo:hi]
 
-        def gather_early(t):
-            nc.vector.tensor_copy(halves[0][:].rearrange("p (c t) -> p c t", t=PACK)[:, :, t], looked_up(t, 0, 2))
+        def gather(t):
+            if t < 3:
+                nc.vector.tensor_copy(halves[0][:].rearrange("p (c t) -> p c t", t=PACK)[:, :, t], looked_up(t, 0, 2))
+            else:
+                for q in range(2):
+                    nc.vector.tensor_copy(picked[q].rearrange("p (c t) -> p c t", t=PACK)[:, :, t], looked_up(t, q, q + 1))
             e = t % 2
-            scalar_cast(flat[t // 2][:, 2 * e * QUARTER : 2 * (e + 1) * QUARTER], looked_up(t, 2, 4))
+            if t < 2:
+                scalar_cast(flat_first[:, 2 * e * QUARTER : 2 * (e + 1) * QUARTER], looked_up(t, 2, 4))
+            else:
+                for q in (2, 3):
+                    scalar_cast(flat_second[q][:, e * QUARTER : (e + 1) * QUARTER], looked_up(t, q, q + 1))
 
-        def gather_last():
-            nc.vector.tensor_copy(halves[0][:].rearrange("p (c t) -> p c t", t=PACK)[:, :, 3], looked_up(3, 0, 2))
-            for q in (2, 3):
-                scalar_cast(flat[1][:, q * QUARTER : (q + 1) * QUARTER], looked_up(3, q, q + 1))
-
-        def weave(q, u):
-            src = flat[u][:].rearrange("p (e c) -> p c e", e=2)[:, (q - 2) * QUARTER : (q - 1) * QUARTER, :]
-            nc.vector.tensor_copy(slot(q, 2 * u, 2 * u + 2), src)
-
-        def cast_x(cast, j, a, z):
+        def cast_x(cast, j, i):
+            lo, hi = BANKS[i]
+            a, z = lo - X_CHUNKS[j][0], hi - X_CHUNKS[j][0]
             cast(
-                x_grouped[j][:, PACK * a : PACK * z].rearrange("p (c i t) -> p c t i", i=4, t=PACK),
-                x_raw[j][:].rearrange("p (t c) -> p t c", t=PACK)[:, :, a:z].rearrange("p t (c i) -> p c t i", i=4),
+                x_grouped[i][:].rearrange("p (c i t) -> p c t i", i=4, t=PACK),
+                x_raw[j][:, :, a:z].rearrange("p t (c i) -> p c t i", i=4),
             )
 
-        def quantize_s(q):
-            lo, hi = 2 * q * QUARTER, 2 * (q + 1) * QUARTER
-            nc.vector.quantize_mx(out=s_codes[:, lo:hi].bitcast(FP8X4), scales=s_bytes[:, lo:hi], in_=halves[q][:])
+        def quantize_s(lo, hi):
+            src = halves[lo // 512][:, PACK * (lo % 512) : PACK * (lo % 512 + hi - lo)]
+            nc.vector.quantize_mx(out=s_codes[:, lo:hi].bitcast(FP8X4), scales=s_bytes[:, lo:hi], in_=src)
 
         def s_pass(i):
-            lo, hi = X_CHUNKS[i]
+            lo, hi = BANKS[i]
             nc.tensor.matmul_mx(
                 out=banks[i][:],
                 lhsT=w2_codes[:].bitcast(FP8X4),
@@ -138,15 +143,11 @@ def tile_picked_recall_bias_e_kernel(tc, xT, sT, w1_words, w1_scales, w2_words, 
             )
 
         def x_quantize(i):
-            lo, hi = X_CHUNKS[i]
+            lo, hi = BANKS[i]
             nc.vector.quantize_mx(out=x_codes[:, lo:hi].bitcast(FP8X4), scales=x_bytes[:, lo:hi], in_=x_grouped[i][:])
 
-        def x_quantize_and_pass(i):
-            x_quantize(i)
-            x_pass(i)
-
         def x_pass(i):
-            lo, hi = X_CHUNKS[i]
+            lo, hi = BANKS[i]
             nc.tensor.matmul_mx(
                 out=banks[i][:],
                 lhsT=w1_codes[:].bitcast(FP8X4),
@@ -159,39 +160,41 @@ def tile_picked_recall_bias_e_kernel(tc, xT, sT, w1_words, w1_scales, w2_words, 
 
         def scalar_read(i):
             nc.scalar.activation(results[i], banks[i][:], IDENTITY, bias=bias)
-            lo, hi = X_CHUNKS[i]
+            lo, hi = BANKS[i]
             nc.sync.dma_start(out[:, lo:hi], results[i])
 
-        gather_early(0)
+        gather(0)
         nc.vector.transpose(bias_cols[:], bias_rows[:])
-        gather_early(1)
-        for q in (2, 3):
-            weave(q, 0)
-        gather_early(2)
-        gather_last()
-        nc.gpsimd.tensor_scalar(
-            x_grouped[0][:].rearrange("p (c t) -> p c t", t=PACK), x_raw[0][:].rearrange("p (t c) -> p c t", t=PACK), 1.0, 0.0, MULT, ADD
+        gather(1)
+        nc.vector.tensor_copy(
+            halves[1][:].rearrange("p (c t) -> p c t", t=PACK)[:, :, 0:2], flat_first[:].rearrange("p (e c) -> p c e", e=2)
         )
-        weave(2, 1)
-        quantize_s(0)
+        gather(2)
+        gather(3)
+        nc.scalar.copy(slot(3, 2, 4), flat_second[3][:].rearrange("p (e c) -> p c e", e=2))
+        nc.vector.tensor_copy(slot(2, 2, 4), flat_second[2][:].rearrange("p (e c) -> p c e", e=2))
+        quantize_s(0, 256)
         s_pass(0)
+        quantize_s(256, 512)
         s_pass(1)
-        weave(3, 1)
-        cast_x(scalar_cast, 1, 0, 256)
-        cast_x(scalar_cast, 2, 0, 256)
-        cast_x(scalar_cast, 3, 0, 128)
-        x_quantize(0)
-        quantize_s(1)
+        quantize_s(512, 1024)
         for i in (2, 3, 4):
             s_pass(i)
-        x_pass(0)
-        x_quantize_and_pass(1)
-        x_quantize_and_pass(2)
-        cast_x(nc.vector.tensor_copy, 3, 128, 256)
-        cast_x(nc.vector.tensor_copy, 4, 0, 128)
-        x_quantize_and_pass(3)
-        x_quantize_and_pass(4)
-        for i in range(4):
+        cast_x(scalar_cast, 0, 0)
+        cast_x(nc.vector.tensor_copy, 0, 1)
+        cast_x(scalar_cast, 1, 2)
+        for i in range(2):
+            x_quantize(i)
+            x_pass(i)
+        cast_x(scalar_cast, 2, 3)
+        x_quantize(2)
+        x_pass(2)
+        cast_x(nc.vector.tensor_copy, 3, 4)
+        for i in (3, 4):
+            x_quantize(i)
+            x_pass(i)
+        for i in range(3):
             scalar_read(i)
-        nc.vector.tensor_scalar_add(results[4], banks[4][:], bias)
-        nc.sync.dma_start(out[:, 896:1024], results[4])
+        for i in (3, 4):
+            nc.vector.tensor_scalar_add(results[i], banks[i][:], bias)
+        nc.sync.dma_start(out[:, 768:1024], result[:, 768:1024])

@@ -44,10 +44,9 @@ def tile_picked_recall_bias_e_kernel(tc, xT, sT, w1_words, w1_scales, w2_words, 
         s_rows = sT.rearrange("(p t) w -> p t w", t=PACK)
         x_rows = xT.rearrange("(p t) w -> p t w", t=PACK)
         planes = [keep.tile([P, T], F32, name=f"plane{t}") for t in range(PACK)]
-        result = keep.tile([P, S], F32, name="result")
-        x_raw = [keep.tile([P, PACK * (hi - lo)], F32, name=f"x_raw{lo}")[:].rearrange("p (t w) -> p t w", t=PACK) for lo, hi in X_CHUNKS[:2]]
-        x_raw.append(result[:].rearrange("p (t w) -> p t w", t=PACK)[:, :, 0:128])
-        x_raw.append(keep.tile([P, PACK * 128], F32, name="x_raw_last")[:].rearrange("p (t w) -> p t w", t=PACK))
+        staging = [keep.tile([P, PACK * (hi - lo)], F32, name=f"x_raw{lo}") for lo, hi in X_CHUNKS]
+        x_raw = [tile[:].rearrange("p (t w) -> p t w", t=PACK) for tile in staging]
+        result = staging[1]
         results = [result[:, lo:hi] for lo, hi in BANKS]
 
         def load_s(t):
@@ -91,7 +90,7 @@ def tile_picked_recall_bias_e_kernel(tc, xT, sT, w1_words, w1_scales, w2_words, 
         }
         s_codes = keep.tile([P, S], U32, name="s_codes", align_bytes=64)
         s_bytes = keep.tile([P, S], U8, name="s_bytes", align_bytes=64)
-        x_grouped = [keep.tile([P, PACK * (hi - lo)], BF16, name=f"x_grouped{lo}", align_bytes=64) for lo, hi in BANKS]
+        x_cast = [keep.tile([P, PACK * (hi - lo)], BF16, name=f"x_cast{lo}", align_bytes=64) for lo, hi in X_CHUNKS]
         x_codes = keep.tile([P, S], U32, name="x_codes", align_bytes=64)
         x_bytes = keep.tile([P, S], U8, name="x_bytes", align_bytes=64)
         banks = [psum.tile([P, hi - lo], F32, name=f"bank{i}") for i, (lo, hi) in enumerate(BANKS)]
@@ -118,12 +117,10 @@ def tile_picked_recall_bias_e_kernel(tc, xT, sT, w1_words, w1_scales, w2_words, 
                 for q in (2, 3):
                     scalar_cast(flat_second[q][:, e * QUARTER : (e + 1) * QUARTER], looked_up(t, q, q + 1))
 
-        def cast_x(cast, j, i):
-            lo, hi = BANKS[i]
-            a, z = lo - X_CHUNKS[j][0], hi - X_CHUNKS[j][0]
+        def cast_x(cast, j, first, last):
             cast(
-                x_grouped[i][:].rearrange("p (c i t) -> p c t i", i=4, t=PACK),
-                x_raw[j][:, :, a:z].rearrange("p t (c i) -> p c t i", i=4),
+                x_cast[j][:, PACK * first : PACK * last].rearrange("p (c i t) -> p c t i", i=4, t=PACK),
+                x_raw[j][:, :, first:last].rearrange("p t (c i) -> p c t i", i=4),
             )
 
         def quantize_s(lo, hi):
@@ -144,7 +141,9 @@ def tile_picked_recall_bias_e_kernel(tc, xT, sT, w1_words, w1_scales, w2_words, 
 
         def x_quantize(i):
             lo, hi = BANKS[i]
-            nc.vector.quantize_mx(out=x_codes[:, lo:hi].bitcast(FP8X4), scales=x_bytes[:, lo:hi], in_=x_grouped[i][:])
+            j = max(n for n, (first, last) in enumerate(X_CHUNKS) if first <= lo)
+            src = x_cast[j][:, PACK * (lo - X_CHUNKS[j][0]) : PACK * (hi - X_CHUNKS[j][0])]
+            nc.vector.quantize_mx(out=x_codes[:, lo:hi].bitcast(FP8X4), scales=x_bytes[:, lo:hi], in_=src)
 
         def x_pass(i):
             lo, hi = BANKS[i]
@@ -180,21 +179,22 @@ def tile_picked_recall_bias_e_kernel(tc, xT, sT, w1_words, w1_scales, w2_words, 
         quantize_s(512, 1024)
         for i in (2, 3, 4):
             s_pass(i)
-        cast_x(scalar_cast, 0, 0)
-        cast_x(nc.vector.tensor_copy, 0, 1)
-        cast_x(scalar_cast, 1, 2)
+        cast_x(scalar_cast, 0, 0, 272)
+        cast_x(nc.vector.tensor_copy, 0, 272, 512)
+        cast_x(scalar_cast, 1, 0, 256)
         for i in range(2):
             x_quantize(i)
             x_pass(i)
-        cast_x(scalar_cast, 2, 3)
+        cast_x(nc.vector.tensor_copy, 2, 0, 128)
         x_quantize(2)
         x_pass(2)
-        cast_x(nc.vector.tensor_copy, 3, 4)
+        cast_x(nc.vector.tensor_copy, 3, 0, 128)
         for i in (3, 4):
             x_quantize(i)
             x_pass(i)
-        for i in range(3):
-            scalar_read(i)
-        for i in (3, 4):
-            nc.vector.tensor_scalar_add(results[i], banks[i][:], bias)
+        scalar_read(0)
+        scalar_read(1)
+        scalar_read(2)
+        nc.scalar.activation(results[3], banks[3][:], IDENTITY, bias=bias)
+        nc.vector.tensor_scalar_add(results[4], banks[4][:], bias)
         nc.sync.dma_start(out[:, 768:1024], result[:, 768:1024])

@@ -21,8 +21,8 @@ PACK = 4
 PER_COLUMN = 16
 QUARTER = S // 4
 
-X_CHUNKS = [(0, 512), (512, 768), (768, 896), (896, 1024)]
-BANKS = [(0, 256), (256, 512), (512, 768), (768, 896), (896, 1024)]
+CHUNKS = [(0, 256), (256, 512), (512, 768), (768, 896), (896, 1024)]
+LOADS = [(0, 512), (512, 768), (768, 896), (896, 1024)]
 
 
 def tile_picked_recall_bias_e_kernel(tc, xT, sT, w1_words, w1_scales, w2_words, w2_scales, b, offs, out):
@@ -44,23 +44,23 @@ def tile_picked_recall_bias_e_kernel(tc, xT, sT, w1_words, w1_scales, w2_words, 
         s_rows = sT.rearrange("(p t) w -> p t w", t=PACK)
         x_rows = xT.rearrange("(p t) w -> p t w", t=PACK)
         planes = [keep.tile([P, T], F32, name=f"plane{t}") for t in range(PACK)]
-        staging = [keep.tile([P, PACK * (hi - lo)], F32, name=f"x_raw{lo}") for lo, hi in X_CHUNKS]
+        staging = [keep.tile([P, PACK * (hi - lo)], F32, name=f"x_raw{lo}") for lo, hi in LOADS]
         x_raw = [tile[:].rearrange("p (t w) -> p t w", t=PACK) for tile in staging]
-        result = staging[1]
-        results = [result[:, lo:hi] for lo, hi in BANKS]
+        results = [keep.tile([P, hi - lo], F32, name=f"result{lo}")[:] for lo, hi in CHUNKS]
+        results = [staging[1][:, lo:hi] for lo, hi in CHUNKS]
 
         def load_s(t):
             nc.sync.dma_start(planes[t][:], s_rows[:, t, :])
 
-        def load_x(j):
-            lo, hi = X_CHUNKS[j]
-            nc.sync.dma_start(x_raw[j], x_rows[:, :, lo:hi])
+        def load_x(n, rows, first, last):
+            lo = LOADS[n][0]
+            nc.sync.dma_start(x_raw[n][:, rows, first - lo : last - lo], x_rows[:, rows, first:last])
 
         def load_codes(codes, words):
             nc.sync.dma_start(codes[:].bitcast(I32), words[0].rearrange("p n t -> p (n t)").bitcast(I32))
 
-        def load_scales(plane, scales):
-            for q in range(P // QUAD):
+        def load_scales(plane, scales, quadrants=range(P // QUAD)):
+            for q in quadrants:
                 nc.sync.dma_start(plane[QUAD * q : QUAD * q + 4, :].bitcast(I32), scales[0, 4 * q : 4 * q + 4, :].bitcast(I32))
 
         nc.vector.memset(bias_rows[:], 0.0)
@@ -70,16 +70,17 @@ def tile_picked_recall_bias_e_kernel(tc, xT, sT, w1_words, w1_scales, w2_words, 
         nc.sync.dma_start(offsets[:], offs)
         load_s(1)
         nc.sync.dma_start(bias_rows[0:P:QUAD, :], b.rearrange("(q j) one -> q (j one)", j=QUAD))
-        load_scales(w2_bytes, w2_scales)
         load_s(2)
-        load_scales(w1_bytes, w1_scales)
         load_s(3)
-        load_x(0)
+        load_scales(w2_bytes, w2_scales)
+        load_scales(w1_bytes, w1_scales, range(0, 1))
+        load_x(0, slice(0, 4), 0, 512)
         load_codes(w2_codes, w2_words)
-        load_x(1)
+        load_scales(w1_bytes, w1_scales, range(1, 4))
+        load_x(1, slice(0, 4), 512, 768)
         load_codes(w1_codes, w1_words)
-        load_x(2)
-        load_x(3)
+        load_x(2, slice(0, 4), 768, 896)
+        load_x(3, slice(0, 4), 896, 1024)
 
         halves = [keep.tile([P, 2 * PACK * QUARTER], BF16, name=f"picked{h}", align_bytes=64) for h in range(2)]
         picked = [halves[q // 2][:, (q % 2) * PACK * QUARTER : (q % 2 + 1) * PACK * QUARTER] for q in range(4)]
@@ -90,10 +91,10 @@ def tile_picked_recall_bias_e_kernel(tc, xT, sT, w1_words, w1_scales, w2_words, 
         }
         s_codes = keep.tile([P, S], U32, name="s_codes", align_bytes=64)
         s_bytes = keep.tile([P, S], U8, name="s_bytes", align_bytes=64)
-        x_cast = [keep.tile([P, PACK * (hi - lo)], BF16, name=f"x_cast{lo}", align_bytes=64) for lo, hi in X_CHUNKS]
+        x_cast = [keep.tile([P, PACK * (hi - lo)], BF16, name=f"x_cast{lo}", align_bytes=64) for lo, hi in LOADS]
         x_codes = keep.tile([P, S], U32, name="x_codes", align_bytes=64)
         x_bytes = keep.tile([P, S], U8, name="x_bytes", align_bytes=64)
-        banks = [psum.tile([P, hi - lo], F32, name=f"bank{i}") for i, (lo, hi) in enumerate(BANKS)]
+        banks = [psum.tile([P, hi - lo], F32, name=f"bank{i}") for i, (lo, hi) in enumerate(CHUNKS)]
 
         def scalar_cast(dst, src):
             nc.scalar.activation(dst, src, COPY)
@@ -117,18 +118,29 @@ def tile_picked_recall_bias_e_kernel(tc, xT, sT, w1_words, w1_scales, w2_words, 
                 for q in (2, 3):
                     scalar_cast(flat_second[q][:, e * QUARTER : (e + 1) * QUARTER], looked_up(t, q, q + 1))
 
-        def cast_x(cast, j, first, last):
+        def load_of(column):
+            return max(n for n, span in enumerate(LOADS) if span[0] <= column)
+
+        def cast_x(cast, first, last):
+            n = load_of(first)
+            lo, hi = first - LOADS[n][0], last - LOADS[n][0]
             cast(
-                x_cast[j][:, PACK * first : PACK * last].rearrange("p (c i t) -> p c t i", i=4, t=PACK),
-                x_raw[j][:, :, first:last].rearrange("p t (c i) -> p c t i", i=4),
+                x_cast[n][:, PACK * lo : PACK * hi].rearrange("p (c i t) -> p c t i", i=4, t=PACK),
+                x_raw[n][:, :, lo:hi].rearrange("p t (c i) -> p c t i", i=4),
             )
+
+        def cast_scalar(first, last):
+            cast_x(scalar_cast, first, last)
+
+        def cast_vector(first, last):
+            cast_x(nc.vector.tensor_copy, first, last)
 
         def quantize_s(lo, hi):
             src = halves[lo // 512][:, PACK * (lo % 512) : PACK * (lo % 512 + hi - lo)]
             nc.vector.quantize_mx(out=s_codes[:, lo:hi].bitcast(FP8X4), scales=s_bytes[:, lo:hi], in_=src)
 
         def s_pass(i):
-            lo, hi = BANKS[i]
+            lo, hi = CHUNKS[i]
             nc.tensor.matmul_mx(
                 out=banks[i][:],
                 lhsT=w2_codes[:].bitcast(FP8X4),
@@ -140,13 +152,13 @@ def tile_picked_recall_bias_e_kernel(tc, xT, sT, w1_words, w1_scales, w2_words, 
             )
 
         def x_quantize(i):
-            lo, hi = BANKS[i]
-            j = max(n for n, (first, last) in enumerate(X_CHUNKS) if first <= lo)
-            src = x_cast[j][:, PACK * (lo - X_CHUNKS[j][0]) : PACK * (hi - X_CHUNKS[j][0])]
+            lo, hi = CHUNKS[i]
+            n = load_of(lo)
+            src = x_cast[n][:, PACK * (lo - LOADS[n][0]) : PACK * (hi - LOADS[n][0])]
             nc.vector.quantize_mx(out=x_codes[:, lo:hi].bitcast(FP8X4), scales=x_bytes[:, lo:hi], in_=src)
 
         def x_pass(i):
-            lo, hi = BANKS[i]
+            lo, hi = CHUNKS[i]
             nc.tensor.matmul_mx(
                 out=banks[i][:],
                 lhsT=w1_codes[:].bitcast(FP8X4),
@@ -157,10 +169,20 @@ def tile_picked_recall_bias_e_kernel(tc, xT, sT, w1_words, w1_scales, w2_words, 
                 stop=True,
             )
 
+        def store(i):
+            lo, hi = CHUNKS[i]
+            if i < 3:
+                nc.sync.dma_start(out[:, lo:hi], results[i])
+            elif i == 4:
+                nc.sync.dma_start(out[:, 768:1024], staging[1][:, 768:1024])
+
         def scalar_read(i):
             nc.scalar.activation(results[i], banks[i][:], IDENTITY, bias=bias)
-            lo, hi = BANKS[i]
-            nc.sync.dma_start(out[:, lo:hi], results[i])
+            store(i)
+
+        def vector_read(i):
+            nc.vector.tensor_scalar_add(results[i], banks[i][:], bias)
+            store(i)
 
         gather(0)
         nc.vector.transpose(bias_cols[:], bias_rows[:])
@@ -179,22 +201,23 @@ def tile_picked_recall_bias_e_kernel(tc, xT, sT, w1_words, w1_scales, w2_words, 
         quantize_s(512, 1024)
         for i in (2, 3, 4):
             s_pass(i)
-        cast_x(scalar_cast, 0, 0, 272)
-        cast_x(nc.vector.tensor_copy, 0, 272, 512)
-        cast_x(scalar_cast, 1, 0, 256)
-        for i in range(2):
-            x_quantize(i)
-            x_pass(i)
-        cast_x(nc.vector.tensor_copy, 2, 0, 128)
+        cast_scalar(0, 272)
+        cast_vector(272, 512)
+        cast_scalar(512, 768)
+        x_quantize(0)
+        x_pass(0)
+        x_quantize(1)
+        x_pass(1)
+        cast_vector(768, 896)
         x_quantize(2)
         x_pass(2)
-        cast_x(nc.vector.tensor_copy, 3, 0, 128)
-        for i in (3, 4):
-            x_quantize(i)
-            x_pass(i)
+        cast_vector(896, 1024)
+        x_quantize(3)
+        x_pass(3)
+        x_quantize(4)
+        x_pass(4)
         scalar_read(0)
         scalar_read(1)
         scalar_read(2)
-        nc.scalar.activation(results[3], banks[3][:], IDENTITY, bias=bias)
-        nc.vector.tensor_scalar_add(results[4], banks[4][:], bias)
-        nc.sync.dma_start(out[:, 768:1024], result[:, 768:1024])
+        scalar_read(3)
+        vector_read(4)

@@ -18,11 +18,16 @@ IDENTITY = mybir.ActivationFunctionType.Identity
 P = 128
 QUAD = 32
 PACK = 4
+SCALE_ROWS = 4
 PER_COLUMN = 16
 QUARTER = S // 4
+HALF = S // 2
+RUN = 4
 
-CHUNKS = [(0, 256), (256, 512), (512, 768), (768, 896), (896, 1024)]
-LOADS = [(0, 512), (512, 768), (768, 896), (896, 1024)]
+X_LOADS = [(0, 512), (512, 768), (768, 896), (896, 1024)]
+BANKS = [(0, 256), (256, 512), (512, 768), (768, 896), (896, 1024)]
+FIRST_SCALAR_SHARE = 272
+RESULT_LOAD = 1
 
 
 def tile_picked_recall_bias_e_kernel(tc, xT, sT, w1_words, w1_scales, w2_words, w2_scales, b, offs, out):
@@ -44,103 +49,98 @@ def tile_picked_recall_bias_e_kernel(tc, xT, sT, w1_words, w1_scales, w2_words, 
         s_rows = sT.rearrange("(p t) w -> p t w", t=PACK)
         x_rows = xT.rearrange("(p t) w -> p t w", t=PACK)
         planes = [keep.tile([P, T], F32, name=f"plane{t}") for t in range(PACK)]
-        staging = [keep.tile([P, PACK * (hi - lo)], F32, name=f"x_raw{lo}") for lo, hi in LOADS]
+        staging = [keep.tile([P, PACK * (hi - lo)], F32, name=f"x_raw{lo}") for lo, hi in X_LOADS]
         x_raw = [tile[:].rearrange("p (t w) -> p t w", t=PACK) for tile in staging]
-        results = [keep.tile([P, hi - lo], F32, name=f"result{lo}")[:] for lo, hi in CHUNKS]
-        results = [staging[1][:, lo:hi] for lo, hi in CHUNKS]
+        result = staging[RESULT_LOAD]
 
-        def load_s(t):
+        def load_plane(t):
             nc.sync.dma_start(planes[t][:], s_rows[:, t, :])
 
-        def load_x(n, rows, first, last):
-            lo = LOADS[n][0]
-            nc.sync.dma_start(x_raw[n][:, rows, first - lo : last - lo], x_rows[:, rows, first:last])
+        def load_x(n):
+            lo, hi = X_LOADS[n]
+            nc.sync.dma_start(x_raw[n], x_rows[:, :, lo:hi])
 
         def load_codes(codes, words):
             nc.sync.dma_start(codes[:].bitcast(I32), words[0].rearrange("p n t -> p (n t)").bitcast(I32))
 
-        def load_scales(plane, scales, quadrants=range(P // QUAD)):
+        def load_scales(w_plane, scales, quadrants):
             for q in quadrants:
-                nc.sync.dma_start(plane[QUAD * q : QUAD * q + 4, :].bitcast(I32), scales[0, 4 * q : 4 * q + 4, :].bitcast(I32))
+                rows = scales[0, SCALE_ROWS * q : SCALE_ROWS * (q + 1), :]
+                nc.sync.dma_start(w_plane[QUAD * q : QUAD * q + SCALE_ROWS, :].bitcast(I32), rows.bitcast(I32))
 
         nc.vector.memset(bias_rows[:], 0.0)
         nc.vector.memset(w_bytes[:].bitcast(I32), 0)
 
-        load_s(0)
+        load_plane(0)
         nc.sync.dma_start(offsets[:], offs)
-        load_s(1)
+        load_plane(1)
         nc.sync.dma_start(bias_rows[0:P:QUAD, :], b.rearrange("(q j) one -> q (j one)", j=QUAD))
-        load_s(2)
-        load_s(3)
-        load_scales(w2_bytes, w2_scales)
+        load_plane(2)
+        load_plane(3)
+        load_scales(w2_bytes, w2_scales, range(0, 4))
         load_scales(w1_bytes, w1_scales, range(0, 1))
-        load_x(0, slice(0, 4), 0, 512)
+        load_x(0)
         load_codes(w2_codes, w2_words)
         load_scales(w1_bytes, w1_scales, range(1, 4))
-        load_x(1, slice(0, 4), 512, 768)
+        load_x(1)
         load_codes(w1_codes, w1_words)
-        load_x(2, slice(0, 4), 768, 896)
-        load_x(3, slice(0, 4), 896, 1024)
+        load_x(2)
+        load_x(3)
 
-        halves = [keep.tile([P, 2 * PACK * QUARTER], BF16, name=f"picked{h}", align_bytes=64) for h in range(2)]
-        picked = [halves[q // 2][:, (q % 2) * PACK * QUARTER : (q % 2 + 1) * PACK * QUARTER] for q in range(4)]
-        flat_first = keep.tile([P, 4 * QUARTER], BF16, name="flat_first", align_bytes=64)
-        flat_second = {
-            2: keep.tile([P, 2 * QUARTER], BF16, name="flat_second2", align_bytes=64),
-            3: keep.tile([P, 2 * QUARTER], BF16, name="flat_second3", align_bytes=64),
-        }
+        halves = [keep.tile([P, PACK * HALF], BF16, name=f"picked{h}", align_bytes=64) for h in range(2)]
+        quarters = [halves[q // 2][:, (q % 2) * PACK * QUARTER : (q % 2 + 1) * PACK * QUARTER] for q in range(4)]
+        runs_01 = keep.tile([P, 2 * HALF], BF16, name="flat_first", align_bytes=64)
+        runs_23 = {q: keep.tile([P, 2 * QUARTER], BF16, name=f"flat_second{q}", align_bytes=64) for q in (2, 3)}
         s_codes = keep.tile([P, S], U32, name="s_codes", align_bytes=64)
         s_bytes = keep.tile([P, S], U8, name="s_bytes", align_bytes=64)
-        x_cast = [keep.tile([P, PACK * (hi - lo)], BF16, name=f"x_cast{lo}", align_bytes=64) for lo, hi in LOADS]
+        x_cast = [keep.tile([P, PACK * (hi - lo)], BF16, name=f"x_cast{lo}", align_bytes=64) for lo, hi in X_LOADS]
         x_codes = keep.tile([P, S], U32, name="x_codes", align_bytes=64)
         x_bytes = keep.tile([P, S], U8, name="x_bytes", align_bytes=64)
-        banks = [psum.tile([P, hi - lo], F32, name=f"bank{i}") for i, (lo, hi) in enumerate(CHUNKS)]
+        banks = [psum.tile([P, hi - lo], F32, name=f"bank{i}") for i, (lo, hi) in enumerate(BANKS)]
 
         def scalar_cast(dst, src):
             nc.scalar.activation(dst, src, COPY)
 
-        def looked_up(t, lo, hi):
-            return planes[t][:].indirect(offsets[:, lo * QUARTER // PER_COLUMN : hi * QUARTER // PER_COLUMN])
+        def looked_up(t, first_quarter, end_quarter):
+            columns = slice(first_quarter * QUARTER // PER_COLUMN, end_quarter * QUARTER // PER_COLUMN)
+            return planes[t][:].indirect(offsets[:, columns])
 
-        def slot(q, lo, hi):
-            return picked[q].rearrange("p (c t) -> p c t", t=PACK)[:, :, lo:hi]
+        def by_row(interleaved):
+            return interleaved.rearrange("p (c t) -> p c t", t=PACK)
+
+        def by_pair(runs):
+            return runs[:].rearrange("p (e c) -> p c e", e=2)
 
         def gather(t):
-            if t < 3:
-                nc.vector.tensor_copy(halves[0][:].rearrange("p (c t) -> p c t", t=PACK)[:, :, t], looked_up(t, 0, 2))
+            if t < PACK - 1:
+                nc.vector.tensor_copy(by_row(halves[0][:])[:, :, t], looked_up(t, 0, 2))
             else:
-                for q in range(2):
-                    nc.vector.tensor_copy(picked[q].rearrange("p (c t) -> p c t", t=PACK)[:, :, t], looked_up(t, q, q + 1))
+                for q in (0, 1):
+                    nc.vector.tensor_copy(by_row(quarters[q])[:, :, t], looked_up(t, q, q + 1))
             e = t % 2
             if t < 2:
-                scalar_cast(flat_first[:, 2 * e * QUARTER : 2 * (e + 1) * QUARTER], looked_up(t, 2, 4))
+                scalar_cast(runs_01[:, e * HALF : (e + 1) * HALF], looked_up(t, 2, 4))
             else:
                 for q in (2, 3):
-                    scalar_cast(flat_second[q][:, e * QUARTER : (e + 1) * QUARTER], looked_up(t, q, q + 1))
+                    scalar_cast(runs_23[q][:, e * QUARTER : (e + 1) * QUARTER], looked_up(t, q, q + 1))
 
         def load_of(column):
-            return max(n for n, span in enumerate(LOADS) if span[0] <= column)
+            return max(n for n, span in enumerate(X_LOADS) if span[0] <= column)
 
-        def cast_x(cast, first, last):
+        def cast_x(cast, first, end):
             n = load_of(first)
-            lo, hi = first - LOADS[n][0], last - LOADS[n][0]
+            lo, hi = first - X_LOADS[n][0], end - X_LOADS[n][0]
             cast(
-                x_cast[n][:, PACK * lo : PACK * hi].rearrange("p (c i t) -> p c t i", i=4, t=PACK),
-                x_raw[n][:, :, lo:hi].rearrange("p t (c i) -> p c t i", i=4),
+                x_cast[n][:, PACK * lo : PACK * hi].rearrange("p (c i t) -> p c t i", i=RUN, t=PACK),
+                x_raw[n][:, :, lo:hi].rearrange("p t (c i) -> p c t i", i=RUN),
             )
 
-        def cast_scalar(first, last):
-            cast_x(scalar_cast, first, last)
-
-        def cast_vector(first, last):
-            cast_x(nc.vector.tensor_copy, first, last)
-
-        def quantize_s(lo, hi):
-            src = halves[lo // 512][:, PACK * (lo % 512) : PACK * (lo % 512 + hi - lo)]
+        def quantize_memories(lo, hi):
+            src = halves[lo // HALF][:, PACK * (lo % HALF) : PACK * (lo % HALF + hi - lo)]
             nc.vector.quantize_mx(out=s_codes[:, lo:hi].bitcast(FP8X4), scales=s_bytes[:, lo:hi], in_=src)
 
-        def s_pass(i):
-            lo, hi = CHUNKS[i]
+        def memory_pass(i):
+            lo, hi = BANKS[i]
             nc.tensor.matmul_mx(
                 out=banks[i][:],
                 lhsT=w2_codes[:].bitcast(FP8X4),
@@ -151,14 +151,11 @@ def tile_picked_recall_bias_e_kernel(tc, xT, sT, w1_words, w1_scales, w2_words, 
                 stop=False,
             )
 
-        def x_quantize(i):
-            lo, hi = CHUNKS[i]
+        def query_pass(i):
+            lo, hi = BANKS[i]
             n = load_of(lo)
-            src = x_cast[n][:, PACK * (lo - LOADS[n][0]) : PACK * (hi - LOADS[n][0])]
+            src = x_cast[n][:, PACK * (lo - X_LOADS[n][0]) : PACK * (hi - X_LOADS[n][0])]
             nc.vector.quantize_mx(out=x_codes[:, lo:hi].bitcast(FP8X4), scales=x_bytes[:, lo:hi], in_=src)
-
-        def x_pass(i):
-            lo, hi = CHUNKS[i]
             nc.tensor.matmul_mx(
                 out=banks[i][:],
                 lhsT=w1_codes[:].bitcast(FP8X4),
@@ -169,55 +166,47 @@ def tile_picked_recall_bias_e_kernel(tc, xT, sT, w1_words, w1_scales, w2_words, 
                 stop=True,
             )
 
-        def store(i):
-            lo, hi = CHUNKS[i]
-            if i < 3:
-                nc.sync.dma_start(out[:, lo:hi], results[i])
-            elif i == 4:
-                nc.sync.dma_start(out[:, 768:1024], staging[1][:, 768:1024])
-
         def scalar_read(i):
-            nc.scalar.activation(results[i], banks[i][:], IDENTITY, bias=bias)
-            store(i)
+            lo, hi = BANKS[i]
+            nc.scalar.activation(result[:, lo:hi], banks[i][:], IDENTITY, bias=bias)
 
         def vector_read(i):
-            nc.vector.tensor_scalar_add(results[i], banks[i][:], bias)
-            store(i)
+            lo, hi = BANKS[i]
+            nc.vector.tensor_scalar_add(result[:, lo:hi], banks[i][:], bias)
+
+        def store(first_bank, last_bank):
+            lo, hi = BANKS[first_bank][0], BANKS[last_bank][1]
+            nc.sync.dma_start(out[:, lo:hi], result[:, lo:hi])
 
         gather(0)
         nc.vector.transpose(bias_cols[:], bias_rows[:])
         gather(1)
-        nc.vector.tensor_copy(
-            halves[1][:].rearrange("p (c t) -> p c t", t=PACK)[:, :, 0:2], flat_first[:].rearrange("p (e c) -> p c e", e=2)
-        )
+        nc.vector.tensor_copy(by_row(halves[1][:])[:, :, 0:2], by_pair(runs_01))
         gather(2)
         gather(3)
-        nc.scalar.copy(slot(3, 2, 4), flat_second[3][:].rearrange("p (e c) -> p c e", e=2))
-        nc.vector.tensor_copy(slot(2, 2, 4), flat_second[2][:].rearrange("p (e c) -> p c e", e=2))
-        quantize_s(0, 256)
-        s_pass(0)
-        quantize_s(256, 512)
-        s_pass(1)
-        quantize_s(512, 1024)
+        nc.scalar.copy(by_row(quarters[3])[:, :, 2:4], by_pair(runs_23[3]))
+        nc.vector.tensor_copy(by_row(quarters[2])[:, :, 2:4], by_pair(runs_23[2]))
+        for i in (0, 1):
+            quantize_memories(*BANKS[i])
+            memory_pass(i)
+        quantize_memories(HALF, S)
         for i in (2, 3, 4):
-            s_pass(i)
-        cast_scalar(0, 272)
-        cast_vector(272, 512)
-        cast_scalar(512, 768)
-        x_quantize(0)
-        x_pass(0)
-        x_quantize(1)
-        x_pass(1)
-        cast_vector(768, 896)
-        x_quantize(2)
-        x_pass(2)
-        cast_vector(896, 1024)
-        x_quantize(3)
-        x_pass(3)
-        x_quantize(4)
-        x_pass(4)
-        scalar_read(0)
-        scalar_read(1)
-        scalar_read(2)
+            memory_pass(i)
+
+        cast_x(scalar_cast, 0, FIRST_SCALAR_SHARE)
+        cast_x(nc.vector.tensor_copy, FIRST_SCALAR_SHARE, X_LOADS[0][1])
+        cast_x(scalar_cast, *X_LOADS[1])
+        query_pass(0)
+        query_pass(1)
+        cast_x(nc.vector.tensor_copy, *X_LOADS[2])
+        query_pass(2)
+        cast_x(nc.vector.tensor_copy, *X_LOADS[3])
+        query_pass(3)
+        query_pass(4)
+
+        for i in (0, 1, 2):
+            scalar_read(i)
+            store(i, i)
         scalar_read(3)
         vector_read(4)
+        store(3, 4)

@@ -24,7 +24,7 @@ QUARTER = S // 4
 HALF = S // 2
 RUN = 4
 
-X_LOADS = [(0, 512), (512, 768), (768, 896), (896, 1024)]
+X_LOADS = [(0, 512), (512, 896), (896, 1024)]
 BANKS = [(0, 256), (256, 512), (512, 768), (768, 896), (896, 1024)]
 FIRST_SCALAR_SHARE = 272
 RESULT_LOAD = 1
@@ -63,10 +63,12 @@ def tile_picked_recall_bias_e_kernel(tc, xT, sT, w1_words, w1_scales, w2_words, 
         def load_codes(codes, words):
             nc.sync.dma_start(codes[:].bitcast(I32), words[0].rearrange("p n t -> p (n t)").bitcast(I32))
 
-        def load_scales(w_plane, scales, quadrants):
-            for q in quadrants:
-                rows = scales[0, SCALE_ROWS * q : SCALE_ROWS * (q + 1), :]
-                nc.sync.dma_start(w_plane[QUAD * q : QUAD * q + SCALE_ROWS, :].bitcast(I32), rows.bitcast(I32))
+        def load_scales(w_plane, scales):
+            nc.sync.dma_start(w_plane[0 : 4 * SCALE_ROWS, :].bitcast(I32), scales[0].bitcast(I32))
+
+        def spread_scales(q):
+            rows = w_bytes[SCALE_ROWS * q : SCALE_ROWS * (q + 1), :]
+            nc.sync.dma_start(w_bytes[QUAD * q : QUAD * q + SCALE_ROWS, :].bitcast(I32), rows.bitcast(I32))
 
         nc.vector.memset(bias_rows[:], 0.0)
         nc.vector.memset(w_bytes[:].bitcast(I32), 0)
@@ -75,17 +77,17 @@ def tile_picked_recall_bias_e_kernel(tc, xT, sT, w1_words, w1_scales, w2_words, 
         nc.sync.dma_start(offsets[:], offs)
         load_plane(1)
         nc.sync.dma_start(bias_rows[0:P:QUAD, :], b.rearrange("(q j) one -> q (j one)", j=QUAD))
+        load_scales(w2_bytes, w2_scales)
+        load_scales(w1_bytes, w1_scales)
         load_plane(2)
         load_plane(3)
-        load_scales(w2_bytes, w2_scales, range(0, 4))
-        load_scales(w1_bytes, w1_scales, range(0, 1))
+        for q in (1, 2, 3):
+            spread_scales(q)
         load_x(0)
         load_codes(w2_codes, w2_words)
-        load_scales(w1_bytes, w1_scales, range(1, 4))
         load_x(1)
         load_codes(w1_codes, w1_words)
         load_x(2)
-        load_x(3)
 
         halves = [keep.tile([P, PACK * HALF], BF16, name=f"picked{h}", align_bytes=64) for h in range(2)]
         quarters = [halves[q // 2][:, (q % 2) * PACK * QUARTER : (q % 2 + 1) * PACK * QUARTER] for q in range(4)]
@@ -195,18 +197,21 @@ def tile_picked_recall_bias_e_kernel(tc, xT, sT, w1_words, w1_scales, w2_words, 
 
         cast_x(scalar_cast, 0, FIRST_SCALAR_SHARE)
         cast_x(nc.vector.tensor_copy, FIRST_SCALAR_SHARE, X_LOADS[0][1])
-        cast_x(scalar_cast, *X_LOADS[1])
         query_pass(0)
         query_pass(1)
-        cast_x(nc.vector.tensor_copy, *X_LOADS[2])
-        query_pass(2)
-        cast_x(nc.vector.tensor_copy, *X_LOADS[3])
+        cast_x(scalar_cast, 512, 640)
+        cast_x(nc.vector.tensor_copy, *BANKS[3])
+        cast_x(nc.vector.tensor_copy, 640, 768)
         query_pass(3)
+        query_pass(2)
+        cast_x(nc.vector.tensor_copy, *X_LOADS[2])
         query_pass(4)
 
-        for i in (0, 1, 2):
+        for i in (0, 1):
             scalar_read(i)
             store(i, i)
         scalar_read(3)
+        scalar_read(2)
+        store(2, 3)
         vector_read(4)
-        store(3, 4)
+        store(4, 4)

@@ -25,7 +25,7 @@ HALF = S // 2
 RUN = 4
 
 X_LOADS = [(0, 512), (512, 896), (896, 1024)]
-BANKS = [(0, 256), (256, 512), (512, 768), (768, 896), (896, 1024)]
+BANKS = [(0, 256), (256, 512), (512, 640), (640, 896), (896, 1024)]
 FIRST_SCALAR_SHARE = 272
 RESULT_LOAD = 1
 
@@ -63,12 +63,10 @@ def tile_picked_recall_bias_e_kernel(tc, xT, sT, w1_words, w1_scales, w2_words, 
         def load_codes(codes, words):
             nc.sync.dma_start(codes[:].bitcast(I32), words[0].rearrange("p n t -> p (n t)").bitcast(I32))
 
-        def load_scales(w_plane, scales):
-            nc.sync.dma_start(w_plane[0 : 4 * SCALE_ROWS, :].bitcast(I32), scales[0].bitcast(I32))
-
-        def spread_scales(q):
-            rows = w_bytes[SCALE_ROWS * q : SCALE_ROWS * (q + 1), :]
-            nc.sync.dma_start(w_bytes[QUAD * q : QUAD * q + SCALE_ROWS, :].bitcast(I32), rows.bitcast(I32))
+        def load_scales(w_plane, scales, quadrants):
+            for q in quadrants:
+                rows = scales[0, SCALE_ROWS * q : SCALE_ROWS * (q + 1), :]
+                nc.sync.dma_start(w_plane[QUAD * q : QUAD * q + SCALE_ROWS, :].bitcast(I32), rows.bitcast(I32))
 
         nc.vector.memset(bias_rows[:], 0.0)
         nc.vector.memset(w_bytes[:].bitcast(I32), 0)
@@ -77,14 +75,13 @@ def tile_picked_recall_bias_e_kernel(tc, xT, sT, w1_words, w1_scales, w2_words, 
         nc.sync.dma_start(offsets[:], offs)
         load_plane(1)
         nc.sync.dma_start(bias_rows[0:P:QUAD, :], b.rearrange("(q j) one -> q (j one)", j=QUAD))
-        load_scales(w2_bytes, w2_scales)
-        load_scales(w1_bytes, w1_scales)
         load_plane(2)
         load_plane(3)
-        for q in (1, 2, 3):
-            spread_scales(q)
+        load_scales(w2_bytes, w2_scales, range(0, 4))
+        load_scales(w1_bytes, w1_scales, range(0, 1))
         load_x(0)
         load_codes(w2_codes, w2_words)
+        load_scales(w1_bytes, w1_scales, range(1, 4))
         load_x(1)
         load_codes(w1_codes, w1_words)
         load_x(2)
@@ -199,19 +196,20 @@ def tile_picked_recall_bias_e_kernel(tc, xT, sT, w1_words, w1_scales, w2_words, 
         cast_x(nc.vector.tensor_copy, FIRST_SCALAR_SHARE, X_LOADS[0][1])
         query_pass(0)
         query_pass(1)
-        cast_x(scalar_cast, 512, 640)
-        cast_x(nc.vector.tensor_copy, *BANKS[3])
-        cast_x(nc.vector.tensor_copy, 640, 768)
-        query_pass(3)
+        cast_x(scalar_cast, 704, 896)
+        cast_x(nc.vector.tensor_copy, *BANKS[2])
+        cast_x(nc.vector.tensor_copy, 640, 704)
         query_pass(2)
         cast_x(nc.vector.tensor_copy, *X_LOADS[2])
+        query_pass(3)
         query_pass(4)
 
-        for i in (0, 1):
-            scalar_read(i)
-            store(i, i)
-        scalar_read(3)
+        scalar_read(0)
+        store(0, 0)
+        scalar_read(1)
         scalar_read(2)
-        store(2, 3)
+        store(1, 2)
+        scalar_read(3)
+        store(3, 3)
         vector_read(4)
         store(4, 4)

from contextlib import ExitStack

import concourse.mybir as mybir

K, T, S, N = 512, 2048, 1024, 128
FLOPS = 2 * 2 * K * S * N

F32 = mybir.dt.float32
BF16 = mybir.dt.bfloat16
I32 = mybir.dt.int32
U32 = mybir.dt.uint32
U16 = mybir.dt.uint16
U8 = mybir.dt.uint8
FP8X4 = mybir.dt.float8_e4m3fn_x4
COPY = mybir.ActivationFunctionType.Copy
IDENTITY = mybir.ActivationFunctionType.Identity

P = 128
QUAD = 32
PACK = 4
SCALE_ROWS = 4
PER_COLUMN = 16
QUARTER = S // 4
HALF = S // 2
RUN = 4

X_LOADS = [(0, 512), (512, 896), (896, 1024)]
BANKS = [(0, 256), (256, 512), (512, 640), (640, 896), (896, 1024)]
FIRST_SCALAR_SHARE = 272
RESULT_LOAD = 1


def tile_picked_recall_bias_e_kernel(tc, xT, sT, w1_words, w1_scales, w2_words, w2_scales, b, offs, out):
    nc = tc.nc
    with ExitStack() as ctx:
        keep = ctx.enter_context(tc.tile_pool(name="keep", bufs=1))
        psum = ctx.enter_context(tc.psum_pool(name="psum", bufs=1))

        offsets = keep.tile([P, S // PER_COLUMN], U16, name="offsets")
        w1_codes = keep.tile([P, N], U32, name="w1_codes", align_bytes=64)
        w2_codes = keep.tile([P, N], U32, name="w2_codes", align_bytes=64)
        w_bytes = keep.tile([P, 2 * N], U8, name="w_bytes", align_bytes=64)
        w1_bytes = w_bytes[:, 0:N]
        w2_bytes = w_bytes[:, N : 2 * N]
        bias_rows = keep.tile([P, QUAD], F32, name="bias_rows", align_bytes=64)
        bias_cols = keep.tile([P, QUAD], F32, name="bias_cols", align_bytes=64)
        bias = bias_cols[:, 0:1]

        s_rows = sT.rearrange("(p t) w -> p t w", t=PACK)
        x_rows = xT.rearrange("(p t) w -> p t w", t=PACK)
        planes = [keep.tile([P, T], F32, name=f"plane{t}") for t in range(PACK)]
        staging = [keep.tile([P, PACK * (hi - lo)], F32, name=f"x_raw{lo}") for lo, hi in X_LOADS]
        x_raw = [tile[:].rearrange("p (t w) -> p t w", t=PACK) for tile in staging]
        result = staging[RESULT_LOAD]

        def load_plane(t):
            nc.sync.dma_start(planes[t][:], s_rows[:, t, :])

        def load_x(n):
            lo, hi = X_LOADS[n]
            nc.sync.dma_start(x_raw[n], x_rows[:, :, lo:hi])

        def load_codes(codes, words):
            nc.sync.dma_start(codes[:].bitcast(I32), words[0].rearrange("p n t -> p (n t)").bitcast(I32))

        def load_scales(w_plane, scales, quadrants):
            for q in quadrants:
                rows = scales[0, SCALE_ROWS * q : SCALE_ROWS * (q + 1), :]
                nc.sync.dma_start(w_plane[QUAD * q : QUAD * q + SCALE_ROWS, :].bitcast(I32), rows.bitcast(I32))

        nc.vector.memset(bias_rows[:], 0.0)
        nc.vector.memset(w_bytes[:].bitcast(I32), 0)

        load_plane(0)
        nc.sync.dma_start(offsets[:], offs)
        load_plane(1)
        nc.sync.dma_start(bias_rows[0:P:QUAD, :], b.rearrange("(q j) one -> q (j one)", j=QUAD))
        load_plane(2)
        load_plane(3)
        load_scales(w2_bytes, w2_scales, range(0, 4))
        load_scales(w1_bytes, w1_scales, range(0, 1))
        load_x(0)
        load_codes(w2_codes, w2_words)
        load_scales(w1_bytes, w1_scales, range(1, 4))
        load_x(1)
        load_codes(w1_codes, w1_words)
        load_x(2)

        halves = [keep.tile([P, PACK * HALF], BF16, name=f"picked{h}", align_bytes=64) for h in range(2)]
        quarters = [halves[q // 2][:, (q % 2) * PACK * QUARTER : (q % 2 + 1) * PACK * QUARTER] for q in range(4)]
        runs_01 = keep.tile([P, 2 * HALF], BF16, name="flat_first", align_bytes=64)
        runs_23 = {q: keep.tile([P, 2 * QUARTER], BF16, name=f"flat_second{q}", align_bytes=64) for q in (2, 3)}
        s_codes = keep.tile([P, S], U32, name="s_codes", align_bytes=64)
        s_bytes = keep.tile([P, S], U8, name="s_bytes", align_bytes=64)
        x_cast = [keep.tile([P, PACK * (hi - lo)], BF16, name=f"x_cast{lo}", align_bytes=64) for lo, hi in X_LOADS]
        x_codes = keep.tile([P, S], U32, name="x_codes", align_bytes=64)
        x_bytes = keep.tile([P, S], U8, name="x_bytes", align_bytes=64)
        banks = [psum.tile([P, hi - lo], F32, name=f"bank{i}") for i, (lo, hi) in enumerate(BANKS)]

        def scalar_cast(dst, src):
            nc.scalar.activation(dst, src, COPY)

        def looked_up(t, first_quarter, end_quarter):
            columns = slice(first_quarter * QUARTER // PER_COLUMN, end_quarter * QUARTER // PER_COLUMN)
            return planes[t][:].indirect(offsets[:, columns])

        def by_row(interleaved):
            return interleaved.rearrange("p (c t) -> p c t", t=PACK)

        def by_pair(runs):
            return runs[:].rearrange("p (e c) -> p c e", e=2)

        def gather(t):
            if t < PACK - 1:
                nc.vector.tensor_copy(by_row(halves[0][:])[:, :, t], looked_up(t, 0, 2))
            else:
                for q in (0, 1):
                    nc.vector.tensor_copy(by_row(quarters[q])[:, :, t], looked_up(t, q, q + 1))
            e = t % 2
            if t < 2:
                scalar_cast(runs_01[:, e * HALF : (e + 1) * HALF], looked_up(t, 2, 4))
            else:
                for q in (2, 3):
                    scalar_cast(runs_23[q][:, e * QUARTER : (e + 1) * QUARTER], looked_up(t, q, q + 1))

        def load_of(column):
            return max(n for n, span in enumerate(X_LOADS) if span[0] <= column)

        def cast_x(cast, first, end):
            n = load_of(first)
            lo, hi = first - X_LOADS[n][0], end - X_LOADS[n][0]
            cast(
                x_cast[n][:, PACK * lo : PACK * hi].rearrange("p (c i t) -> p c t i", i=RUN, t=PACK),
                x_raw[n][:, :, lo:hi].rearrange("p t (c i) -> p c t i", i=RUN),
            )

        def quantize_memories(lo, hi):
            src = halves[lo // HALF][:, PACK * (lo % HALF) : PACK * (lo % HALF + hi - lo)]
            nc.vector.quantize_mx(out=s_codes[:, lo:hi].bitcast(FP8X4), scales=s_bytes[:, lo:hi], in_=src)

        def memory_pass(i):
            lo, hi = BANKS[i]
            nc.tensor.matmul_mx(
                out=banks[i][:],
                lhsT=w2_codes[:].bitcast(FP8X4),
                lhsT_scale=w2_bytes,
                rhs=s_codes[:, lo:hi].bitcast(FP8X4),
                rhs_scale=s_bytes[:, lo:hi],
                start=True,
                stop=False,
            )

        def query_pass(i):
            lo, hi = BANKS[i]
            n = load_of(lo)
            src = x_cast[n][:, PACK * (lo - X_LOADS[n][0]) : PACK * (hi - X_LOADS[n][0])]
            nc.vector.quantize_mx(out=x_codes[:, lo:hi].bitcast(FP8X4), scales=x_bytes[:, lo:hi], in_=src)
            nc.tensor.matmul_mx(
                out=banks[i][:],
                lhsT=w1_codes[:].bitcast(FP8X4),
                lhsT_scale=w1_bytes,
                rhs=x_codes[:, lo:hi].bitcast(FP8X4),
                rhs_scale=x_bytes[:, lo:hi],
                start=False,
                stop=True,
            )

        def scalar_read(i):
            lo, hi = BANKS[i]
            nc.scalar.activation(result[:, lo:hi], banks[i][:], IDENTITY, bias=bias)

        def vector_read(i):
            lo, hi = BANKS[i]
            nc.vector.tensor_scalar_add(result[:, lo:hi], banks[i][:], bias)

        def store(first_bank, last_bank):
            lo, hi = BANKS[first_bank][0], BANKS[last_bank][1]
            nc.sync.dma_start(out[:, lo:hi], result[:, lo:hi])

        gather(0)
        nc.vector.transpose(bias_cols[:], bias_rows[:])
        gather(1)
        nc.vector.tensor_copy(by_row(halves[1][:])[:, :, 0:2], by_pair(runs_01))
        gather(2)
        gather(3)
        nc.scalar.copy(by_row(quarters[3])[:, :, 2:4], by_pair(runs_23[3]))
        nc.vector.tensor_copy(by_row(quarters[2])[:, :, 2:4], by_pair(runs_23[2]))
        for i in (0, 1):
            quantize_memories(*BANKS[i])
            memory_pass(i)
        quantize_memories(HALF, S)
        for i in (2, 3, 4):
            memory_pass(i)

        cast_x(scalar_cast, 0, FIRST_SCALAR_SHARE)
        cast_x(nc.vector.tensor_copy, FIRST_SCALAR_SHARE, X_LOADS[0][1])
        query_pass(0)
        query_pass(1)
        cast_x(scalar_cast, 704, 896)
        cast_x(nc.vector.tensor_copy, *BANKS[2])
        cast_x(nc.vector.tensor_copy, 640, 704)
        query_pass(2)
        cast_x(nc.vector.tensor_copy, *X_LOADS[2])
        query_pass(3)
        query_pass(4)

        scalar_read(0)
        store(0, 0)
        scalar_read(1)
        scalar_read(2)
        store(1, 2)
        scalar_read(3)
        store(3, 3)
        vector_read(4)
        store(4, 4)
